import numpy as np
import ml_dtypes


def mxq(x, axis, fmt="e4m3"):
    dtype, down = {"e4m3": (ml_dtypes.float8_e4m3fn, 7), "e5m2": (ml_dtypes.float8_e5m2, 14)}[fmt]
    v = np.moveaxis(np.asarray(x, np.float32).astype(ml_dtypes.bfloat16).astype(np.float64), axis, -1)
    blocks = v.reshape(v.shape[:-1] + (-1, 32))
    amax = np.abs(blocks).max(-1, keepdims=True)
    byte = np.maximum(np.where(amax > 0, np.frexp(amax)[1] - 1 + 127, 0) - down, 1)
    scale = np.exp2(byte - 127.0)
    codes = (blocks / scale).astype(np.float32).astype(dtype).astype(np.float64)
    return np.moveaxis((codes * scale).reshape(v.shape), -1, axis)


WIDE = False


def mx_kscale(k):
    if not WIDE:
        return np.ones(k)
    levels = np.array([24, -24, 12, -12, 0])
    if k % 512:
        return np.exp2(np.random.permutation(np.resize(levels, k // 32))).repeat(32)
    a = np.empty((k // 512, 16))
    for p in range(k // 512):
        a[p, :8] = np.random.permutation(np.resize(levels, 8))
        for g in range(8):
            far = levels[np.abs(levels - a[p, g]) >= 10]
            a[p, g + 8] = far[np.random.randint(len(far))]
    return np.exp2(a.ravel()).repeat(32)


def f64(x):
    return np.asarray(x).astype(np.float64)


def striped(idx):
    return np.tile(idx.reshape(-1, 16).T, (8, 1)).astype(np.uint16)


def unstriped(offs):
    return offs[:16].T.reshape(-1).astype(np.int64)


E2M1 = np.array([0.0, 0.5, 1.0, 1.5, 2.0, 3.0, 4.0, 6.0, -0.0, -0.5, -1.0, -1.5, -2.0, -3.0, -4.0, -6.0])


def pack_weight(w, fmt):
    k, n = w.shape
    w = f64(np.asarray(w, np.float32).astype(ml_dtypes.bfloat16)).reshape(k // 32, 32, n)
    amax = np.abs(w).max(1)
    if fmt == "e4m3":
        byte = np.frexp(amax)[1] - 1 + 127 - 7
    else:
        mant, ex = np.frexp(amax / 6.0)
        byte = np.where(mant > 0.5, ex, ex - 1) + 127
    byte = np.clip(np.where(amax > 0, byte, 1), 1, 254)
    scaled = (w * np.exp2(127.0 - byte)[:, None, :]).reshape(k, n).astype(np.float32)
    by_word = np.ascontiguousarray(scaled.reshape(k // 512, 128, 4, n).transpose(0, 1, 3, 2))
    if fmt == "e4m3":
        words = by_word.astype(ml_dtypes.float8_e4m3fn).view(np.uint8)
    else:
        c = by_word.astype(ml_dtypes.float4_e2m1fn).view(np.uint8) & 0xF
        words = (c[..., 0::2] | (c[..., 1::2] << 4)).reshape(k // 512, 128, 2 * n)
    return np.ascontiguousarray(words), np.ascontiguousarray(byte.astype(np.uint8).reshape(k // 512, 16, n))


def unpack_weight(words, scales, fmt):
    g, _, n = scales.shape
    words = np.ascontiguousarray(words).reshape(g, 128, n, -1)
    if fmt == "e4m3":
        vals = words.view(ml_dtypes.float8_e4m3fn).astype(np.float64)
    else:
        nib = np.empty((g, 128, n, 4), np.uint8)
        nib[..., 0::2] = words & 0xF
        nib[..., 1::2] = words >> 4
        vals = E2M1[nib]
    vals = vals * np.repeat(np.exp2(scales.astype(np.float64) - 127.0), 8, axis=1)[..., None]
    return vals.transpose(0, 1, 3, 2).reshape(g * 512, n)


def pack_table4(v):
    words, scales = pack_weight(v, "e2m1")
    g, t = words.shape[0] // 2, v.shape[1]
    return np.ascontiguousarray(words.reshape(g, 2, 128, t, 2).transpose(0, 2, 3, 1, 4).reshape(g, 128, t, 4)), scales


def unpack_table4(words, scales):
    g, _, t, _ = words.shape
    return unpack_weight(words.reshape(g, 128, t, 2, 2).transpose(0, 3, 1, 2, 4).reshape(2 * g, 128, 2 * t), scales, "e2m1")


def planes(y):
    n, m = y.shape
    v = y.astype(np.float32).astype(ml_dtypes.bfloat16).astype(np.float64).reshape(n // 32, 32, m)
    top = np.abs(v).max(1)
    byte = np.clip(np.where(top > 0, np.frexp(top)[1] - 1 + 127 - 7, 1), 1, 254)
    codes = (v * np.exp2(127.0 - byte)[:, None, :]).reshape(n, m).astype(np.float32).astype(ml_dtypes.float8_e4m3fn).view(np.uint8)
    words = codes.reshape(n // 512, 128, 4, m).transpose(0, 1, 3, 2)
    return np.ascontiguousarray(words), np.ascontiguousarray(byte.astype(np.uint8).reshape(n // 512, 16, m))


def gelu(f):
    return 0.5 * f * (1.0 + np.tanh(np.sqrt(2.0 / np.pi) * (f + 0.044715 * f**3)))


K, R, N, T, J = 1024, 512, 512, 4096, 1024


def setup_inputs():
    n = np.random.standard_normal
    s = mx_kscale(K)[:, None]
    u = mx_kscale(R)[:, None]
    p_tab = pack_table4(n((K, T)) * s)
    p_wg = pack_weight(n((K, R)) / np.sqrt(K) / s, "e4m3")
    p_wu = pack_weight(n((K, R)) / np.sqrt(K) / s * u.T, "e4m3")
    p_wd = pack_weight(n((R, N)) / np.sqrt(R) / u, "e2m1")
    return {
        "tab_words": p_tab[0],
        "tab_scales": p_tab[1],
        "wg_words": p_wg[0],
        "wg_scales": p_wg[1],
        "wu_words": p_wu[0],
        "wu_scales": p_wu[1],
        "wd_words": p_wd[0],
        "wd_scales": p_wd[1],
        "gT": (n((N, T))).astype(np.float32),
        "offs": striped(np.random.permutation(T)[:J]),
    }


def reference(tab_words, tab_scales, wg_words, wg_scales, wu_words, wu_scales, wd_words, wd_scales, gT, offs):
    idx = unstriped(offs)
    tab_ = unpack_table4(tab_words, tab_scales)[:, idx]
    wg_ = unpack_weight(wg_words, wg_scales, "e4m3")
    wu_ = unpack_weight(wu_words, wu_scales, "e4m3")
    ga = wg_.T @ tab_
    ub = wu_.T @ tab_
    h = gelu(ga) * ub
    h_ = mxq(h, 0, "e4m3")
    wd_ = unpack_weight(wd_words, wd_scales, "e2m1")
    y = wd_.T @ h_
    out_0 = y * f64(gT)[:, idx]
    return (out_0,) + planes(out_0)

@@ -1,0 +1,206 @@
+from contextlib import ExitStack
+
+import concourse.mybir as mybir
+from concourse.masks import make_identity
+
+K, R, N, T, J = 1024, 512, 512, 4096, 1024
+FLOPS = 2 * J * (2 * K * R + R * N)
+
+F32 = mybir.dt.float32
+BF16 = mybir.dt.bfloat16
+I32 = mybir.dt.int32
+U32 = mybir.dt.uint32
+U16 = mybir.dt.uint16
+U8 = mybir.dt.uint8
+FP8X4 = mybir.dt.float8_e4m3fn_x4
+FP4X4 = mybir.dt.float4_e2m1fn_x4
+MULT = mybir.AluOpType.mult
+GELU = mybir.ActivationFunctionType.Gelu_apprx_tanh
+
+P = 128
+PASSES = K // 512
+HALF = 512
+HALVES = J // HALF
+CHUNK = 256
+CHUNKS = J // CHUNK
+
+
+def tile_list_gmlpt_gelu_gateP_kernel(
+    tc, tab_words, tab_scales, wg_words, wg_scales, wu_words, wu_scales, wd_words, wd_scales, gT, offs, out_0, out_1, out_2
+):
+    nc = tc.nc
+    with ExitStack() as ctx:
+        held = ctx.enter_context(tc.tile_pool(name="held", bufs=1))
+        ring = ctx.enter_context(tc.tile_pool(name="ring", bufs=3))
+        psum = ctx.enter_context(tc.psum_pool(name="psum", bufs=2))
+
+        offsets = held.tile([P, J // 16], U16, name="offsets")
+        nc.sync.dma_start(offsets[:], offs)
+
+        def entries(start, count):
+            return offsets[:, start // 16 : (start + count) // 16]
+
+        table_scales = held.tile([P, T], U8, name="table_scales", tag="slot_wu", align_bytes=64)
+        nc.sync.dma_start(table_scales[0:32, :].bitcast(I32), tab_scales.rearrange("a q t -> (a q) t").bitcast(I32))
+        nc.vector.memset(table_scales[32:64, :].bitcast(I32), 0)
+        nc.vector.memset(table_scales[64:128, :].bitcast(I32), 0)
+
+        staged = held.tile([P, 2 * PASSES + 1, R], U8, name="staged")
+        for first, count, scales in ((0, PASSES, wg_scales), (PASSES, PASSES, wu_scales), (2 * PASSES, 1, wd_scales)):
+            nc.sync.dma_start(
+                staged[0:P:8, first : first + count, :].bitcast(I32), scales.rearrange("a q n -> q a n").bitcast(I32)
+            )
+        wd_raw = held.tile([P, N // 2], I32, name="wd_raw", tag="slot_wg", align_bytes=64)
+        nc.sync.dma_start(wd_raw[:], wd_words[0].bitcast(I32))
+        table = held.tile([P, T], I32, name="table", tag="slot2")
+        nc.sync.dma_start(table[:], tab_words[0].rearrange("p t b -> p (t b)").bitcast(I32))
+        wd = held.tile([P, 4, 2 * P], U8, name="wd", align_bytes=64)
+        nc.vector.tensor_copy(wd[:].bitcast(U16), wd_raw[:].bitcast(U16).rearrange("p (m t) -> p t m", t=4))
+
+        weight_scales = held.tile([P, 2 * PASSES + 1, R], U8, name="weight_scales", align_bytes=64)
+        nc.vector.memset(weight_scales[:].bitcast(I32), 0)
+        picked_scales = held.tile([P, PASSES, J], U8, name="picked_scales", align_bytes=64)
+        nc.vector.memset(picked_scales[:].bitcast(I32), 0)
+        for q in range(4):
+            nc.scalar.dma_start(
+                weight_scales[32 * q : 32 * q + 4, :, :].bitcast(I32), staged[32 * q : 32 * q + 32 : 8, :, :].bitcast(I32)
+            )
+
+        identity = held.tile([P, P], F32, name="identity")
+        make_identity(nc, identity[:])
+
+        warm = held.tile([P, 8], F32, name="warm")
+        nc.vector.memset(warm[:, 0:4], 0.0)
+        nc.scalar.activation(warm[:, 4:8], warm[:, 0:4], GELU)
+
+        picked_rows = held.tile([P, J], U8, name="picked_rows", tag="slot3")
+        nc.vector.tensor_copy(picked_rows[:], table_scales[:].indirect(offsets[:]))
+        for a in range(PASSES):
+            for q in range(4):
+                row = 16 * a + 4 * q
+                nc.scalar.dma_start(
+                    picked_scales[32 * q : 32 * q + 4, a, :].bitcast(I32), picked_rows[row : row + 4, :].bitcast(I32)
+                )
+
+        up_weights = []
+        for name, words in (("wg", wg_words), ("wu", wu_words)):
+            w = held.tile([P, PASSES, R], I32, name=name, tag="slot_" + name, align_bytes=64)
+            nc.sync.dma_start(w[:], words.rearrange("a p r i -> p a (r i)").bitcast(I32))
+            up_weights.append(w)
+
+        picked_words = []
+        for hf in range(HALVES):
+            listed = entries(hf * HALF, HALF)
+            pairs = held.tile([P, HALF], U32, name="picked_pairs%d" % hf, tag="slot%d" % hf)
+            nc.vector.tensor_copy(pairs[:], table[:].bitcast(U32).indirect(listed))
+            words = held.tile([P, PASSES, 2 * HALF], U8, name="picked_words%d" % hf, align_bytes=64)
+            nc.vector.tensor_copy(
+                words[:].bitcast(U16), pairs[:].bitcast(U16).rearrange("p (j a) -> p a j", a=PASSES)
+            )
+            picked_words.append(words)
+
+        gate_rows = gT.rearrange("(p t) c -> t p c", t=4)
+        gates = []
+        for t in range(4):
+            g = held.tile([P, T], F32, name="gate%d" % t, tag="slot%d" % t)
+            nc.sync.dma_start(g[:], gate_rows[t])
+            gates.append(g)
+
+        wd_scale = held.tile([P, 4, P], U8, name="wd_scale", align_bytes=64)
+        nc.vector.tensor_copy(wd_scale[:], weight_scales[:, 2 * PASSES, :].rearrange("p (m t) -> p t m", t=4))
+
+        picked_gates = [held.tile([P, HALF], F32, name="picked_gates%d" % hf) for hf in range(HALVES)]
+        y_rows = [held.tile([P, 4, CHUNK], F32, name="y_rows%d" % c) for c in range(CHUNKS)]
+        early = held.tile([P, 2, J], F32, name="early")
+        late = [held.tile([P, 2, CHUNK], F32, name="late%d" % c) for c in range(CHUNKS)]
+        rounded = [held.tile([P, CHUNK, 4], BF16, name="rounded%d" % c, align_bytes=64) for c in range(CHUNKS)]
+        out_codes = [held.tile([P, HALF], I32, name="out_codes%d" % hf, align_bytes=64) for hf in range(HALVES)]
+        out_scales = held.tile([P, J], U8, name="out_scales", align_bytes=64)
+
+        def first_stage(jt):
+            hf, col = divmod(jt * P, HALF)
+            sums = []
+            for m in range(2):
+                acc = psum.tile([P, R], F32, name="sum%d" % m, bufs=2 + m)
+                for a in range(PASSES):
+                    nc.tensor.matmul_mx(
+                        out=acc[:],
+                        lhsT=picked_words[hf][:, a, 2 * col : 2 * (col + P)].bitcast(FP4X4),
+                        lhsT_scale=picked_scales[:, a, jt * P : (jt + 1) * P],
+                        rhs=up_weights[m][:, a, :].bitcast(FP8X4),
+                        rhs_scale=weight_scales[:, m * PASSES + a, :],
+                        start=(a == 0),
+                        stop=(a == PASSES - 1),
+                    )
+                sums.append(acc[:].rearrange("p (m u e) -> p u m e", u=2, e=2))
+            activated = ring.tile([P, 2, P, 2], F32, name="activated")
+            nc.scalar.activation(activated[:], sums[0], GELU)
+            h = ring.tile([P, 2, P, 2], BF16, name="h", bufs=4)
+            nc.vector.tensor_tensor(h[:], sums[1], activated[:], MULT)
+            return h
+
+        def turn(pair, grouped):
+            turned = psum.tile([P, 2, 2, P], F32, name="turned", bufs=1)
+            for i, h in enumerate(pair):
+                words = h[:].rearrange("p u m e -> p (u m e)").bitcast(F32)
+                for u in range(2):
+                    nc.tensor.transpose(turned[:, i, u, :], words[:, u * P : (u + 1) * P], identity[:])
+            nc.scalar.copy(grouped.rearrange("p (i j) u -> p i j u", i=2), turned[:].rearrange("p i u j -> p i j u"))
+
+        def second_stage(c, codes, scales):
+            for first in (0, 2):
+                y = psum.tile([P, 2, CHUNK], F32, name="y", bufs=2)
+                for i in range(2):
+                    nc.tensor.matmul_mx(
+                        out=y[:, i, :],
+                        lhsT=wd[:, first + i, :].bitcast(FP4X4),
+                        lhsT_scale=wd_scale[:, first + i, :],
+                        rhs=codes[:].bitcast(FP8X4),
+                        rhs_scale=scales[:],
+                        start=True,
+                        stop=True,
+                    )
+                nc.scalar.copy(y_rows[c][:, first : first + 2, :], y[:])
+
+        for c in range(CHUNKS):
+            grouped = ring.tile([P, CHUNK, 2], F32, name="grouped", align_bytes=64, bufs=2)
+            codes = ring.tile([P, CHUNK], U32, name="h_codes", align_bytes=64, bufs=2)
+            scales = ring.tile([P, CHUNK], U8, name="h_scales", align_bytes=64, bufs=2)
+            turn([first_stage(2 * c), first_stage(2 * c + 1)], grouped[:])
+            nc.vector.quantize_mx(
+                out=codes[:].bitcast(FP8X4),
+                scales=scales[:],
+                in_=grouped[:].rearrange("p j u -> p (j u)").bitcast(BF16),
+            )
+            second_stage(c, codes, scales)
+
+        out_rows = out_0.rearrange("(p t) j -> p t j", t=4)
+        for hf in range(HALVES):
+            nc.vector.tensor_copy(picked_gates[hf][:], gates[0][:].indirect(entries(hf * HALF, HALF)))
+        for c in range(CHUNKS):
+            cols = slice(c * CHUNK, (c + 1) * CHUNK)
+            hf, col = divmod(c * CHUNK, HALF)
+            nc.vector.tensor_tensor(early[:, 0, cols], picked_gates[hf][:, col : col + CHUNK], y_rows[c][:, 0, :], MULT)
+            nc.vector.tensor_tensor(early[:, 1, cols], gates[1][:].indirect(entries(c * CHUNK, CHUNK)), y_rows[c][:, 1, :], MULT)
+            nc.scalar.copy(rounded[c][:, :, 0:2], early[:, :, cols].rearrange("p t j -> p j t"))
+        nc.sync.dma_start(out_rows[:, 0:2, :], early[:])
+        for t in (2, 3):
+            for c in range(CHUNKS):
+                nc.vector.tensor_tensor(
+                    late[c][:, t - 2, :], gates[t][:].indirect(entries(c * CHUNK, CHUNK)), y_rows[c][:, t, :], MULT
+                )
+        word_rows = out_1[0].rearrange("p j i -> p (j i)").bitcast(I32)
+        for c in range(CHUNKS):
+            cols = slice(c * CHUNK, (c + 1) * CHUNK)
+            hf, col = divmod(c * CHUNK, HALF)
+            nc.sync.dma_start(out_rows[:, 2:4, cols], late[c][:])
+            nc.scalar.copy(rounded[c][:, :, 2:4], late[c][:].rearrange("p t j -> p j t"))
+            nc.vector.quantize_mx(
+                out=out_codes[hf][:, col : col + CHUNK].bitcast(FP8X4),
+                scales=out_scales[:, cols],
+                in_=rounded[c][:].rearrange("p j t -> p (j t)"),
+            )
+            if col + CHUNK == HALF:
+                nc.sync.dma_start(word_rows[:, hf * HALF : (hf + 1) * HALF], out_codes[hf][:])
+        for q in range(4):
+            nc.scalar.dma_start(out_2[0, 4 * q : 4 * q + 4, :].bitcast(I32), out_scales[32 * q : 32 * q + 4, :].bitcast(I32))

@@ -31,6 +31,7 @@ def tile_list_gmlpt_gelu_gateP_kernel(
     nc = tc.nc
     with ExitStack() as ctx:
         held = ctx.enter_context(tc.tile_pool(name="held", bufs=1))
+        reused = ctx.enter_context(tc.tile_pool(name="reused", bufs=1))
         ring = ctx.enter_context(tc.tile_pool(name="ring", bufs=3))
         psum = ctx.enter_context(tc.psum_pool(name="psum", bufs=2))
 
@@ -40,7 +41,10 @@ def tile_list_gmlpt_gelu_gateP_kernel(
         def entries(start, count):
             return offsets[:, start // 16 : (start + count) // 16]
 
-        table_scales = held.tile([P, T], U8, name="table_scales", tag="slot_wu", align_bytes=64)
+        table = held.tile([P, T], I32, name="table", tag="slot1", align_bytes=64)
+        nc.gpsimd.dma_start(table[:], tab_words[0].rearrange("p t b -> p (t b)").bitcast(I32))
+
+        table_scales = reused.tile([P, T], U8, name="table_scales", offset=6144)
         nc.sync.dma_start(table_scales[0:32, :].bitcast(I32), tab_scales.rearrange("a q t -> (a q) t").bitcast(I32))
         nc.vector.memset(table_scales[32:64, :].bitcast(I32), 0)
         nc.vector.memset(table_scales[64:128, :].bitcast(I32), 0)
@@ -50,17 +54,16 @@ def tile_list_gmlpt_gelu_gateP_kernel(
             nc.sync.dma_start(
                 staged[0:P:8, first : first + count, :].bitcast(I32), scales.rearrange("a q n -> q a n").bitcast(I32)
             )
-        wd_raw = held.tile([P, N // 2], I32, name="wd_raw", tag="slot_wg", align_bytes=64)
+        wd_raw = held.tile([P, N // 2], I32, name="wd_raw")
         nc.sync.dma_start(wd_raw[:], wd_words[0].bitcast(I32))
-        table = held.tile([P, T], I32, name="table", tag="slot2")
-        nc.sync.dma_start(table[:], tab_words[0].rearrange("p t b -> p (t b)").bitcast(I32))
         wd = held.tile([P, 4, 2 * P], U8, name="wd", align_bytes=64)
         nc.vector.tensor_copy(wd[:].bitcast(U16), wd_raw[:].bitcast(U16).rearrange("p (m t) -> p t m", t=4))
 
         weight_scales = held.tile([P, 2 * PASSES + 1, R], U8, name="weight_scales", align_bytes=64)
         nc.vector.memset(weight_scales[:].bitcast(I32), 0)
-        picked_scales = held.tile([P, PASSES, J], U8, name="picked_scales", align_bytes=64)
-        nc.vector.memset(picked_scales[:].bitcast(I32), 0)
+        picked_scales = [held.tile([P, J], U8, name="picked_scales%d" % a, align_bytes=64) for a in range(PASSES)]
+        for plane in picked_scales:
+            nc.vector.memset(plane[:].bitcast(I32), 0)
         for q in range(4):
             nc.scalar.dma_start(
                 weight_scales[32 * q : 32 * q + 4, :, :].bitcast(I32), staged[32 * q : 32 * q + 32 : 8, :, :].bitcast(I32)
@@ -73,25 +76,26 @@ def tile_list_gmlpt_gelu_gateP_kernel(
         nc.vector.memset(warm[:, 0:4], 0.0)
         nc.scalar.activation(warm[:, 4:8], warm[:, 0:4], GELU)
 
-        picked_rows = held.tile([P, J], U8, name="picked_rows", tag="slot3")
+        picked_rows = held.tile([P, J], U8, name="picked_rows", tag="slot3", align_bytes=64)
         nc.vector.tensor_copy(picked_rows[:], table_scales[:].indirect(offsets[:]))
-        for a in range(PASSES):
-            for q in range(4):
-                row = 16 * a + 4 * q
-                nc.scalar.dma_start(
-                    picked_scales[32 * q : 32 * q + 4, a, :].bitcast(I32), picked_rows[row : row + 4, :].bitcast(I32)
-                )
 
-        up_weights = []
-        for name, words in (("wg", wg_words), ("wu", wu_words)):
-            w = held.tile([P, PASSES, R], I32, name=name, tag="slot_" + name, align_bytes=64)
-            nc.sync.dma_start(w[:], words.rearrange("a p r i -> p a (r i)").bitcast(I32))
-            up_weights.append(w)
+        def move_scale_rows(a, q):
+            row = 16 * a + 4 * q
+            nc.sync.dma_start(picked_scales[a][32 * q : 32 * q + 4, :].bitcast(I32), picked_rows[row : row + 4, :].bitcast(I32))
+
+        moves = [(a, q) for a in range(PASSES) for q in range(4)]
+        for a, q in moves[:6]:
+            move_scale_rows(a, q)
+        up_weights = reused.tile([P, 2, PASSES, R], I32, name="up_weights", offset=0, align_bytes=64)
+        for m, words in enumerate((wg_words, wu_words)):
+            nc.sync.dma_start(up_weights[:, m, :, :], words.rearrange("a p r i -> p a (r i)").bitcast(I32))
+        for a, q in moves[6:]:
+            move_scale_rows(a, q)
 
         picked_words = []
         for hf in range(HALVES):
             listed = entries(hf * HALF, HALF)
-            pairs = held.tile([P, HALF], U32, name="picked_pairs%d" % hf, tag="slot%d" % hf)
+            pairs = held.tile([P, HALF], U32, name="picked_pairs%d" % hf, tag="slot2", align_bytes=64)
             nc.vector.tensor_copy(pairs[:], table[:].bitcast(U32).indirect(listed))
             words = held.tile([P, PASSES, 2 * HALF], U8, name="picked_words%d" % hf, align_bytes=64)
             nc.vector.tensor_copy(
@@ -100,21 +104,17 @@ def tile_list_gmlpt_gelu_gateP_kernel(
             picked_words.append(words)
 
         gate_rows = gT.rearrange("(p t) c -> t p c", t=4)
-        gates = []
+        gates = [reused.tile([P, T], F32, name="gate0", offset=8192)]
+        gates.extend(held.tile([P, T], F32, name="gate%d" % t, tag="slot%d" % t, align_bytes=64) for t in range(1, 4))
         for t in range(4):
-            g = held.tile([P, T], F32, name="gate%d" % t, tag="slot%d" % t)
-            nc.sync.dma_start(g[:], gate_rows[t])
-            gates.append(g)
+            nc.sync.dma_start(gates[t][:], gate_rows[t])
 
         wd_scale = held.tile([P, 4, P], U8, name="wd_scale", align_bytes=64)
         nc.vector.tensor_copy(wd_scale[:], weight_scales[:, 2 * PASSES, :].rearrange("p (m t) -> p t m", t=4))
 
-        picked_gates = [held.tile([P, HALF], F32, name="picked_gates%d" % hf) for hf in range(HALVES)]
         y_rows = [held.tile([P, 4, CHUNK], F32, name="y_rows%d" % c) for c in range(CHUNKS)]
-        early = held.tile([P, 2, J], F32, name="early")
-        late = [held.tile([P, 2, CHUNK], F32, name="late%d" % c) for c in range(CHUNKS)]
-        rounded = [held.tile([P, CHUNK, 4], BF16, name="rounded%d" % c, align_bytes=64) for c in range(CHUNKS)]
-        out_codes = [held.tile([P, HALF], I32, name="out_codes%d" % hf, align_bytes=64) for hf in range(HALVES)]
+        products = [held.tile([P, 4, CHUNK], F32, name="products%d" % c) for c in range(CHUNKS)]
+        out_codes = [held.tile([P, CHUNK], I32, name="out_codes%d" % c, align_bytes=64) for c in range(CHUNKS)]
         out_scales = held.tile([P, J], U8, name="out_scales", align_bytes=64)
 
         def first_stage(jt):
@@ -126,16 +126,16 @@ def tile_list_gmlpt_gelu_gateP_kernel(
                     nc.tensor.matmul_mx(
                         out=acc[:],
                         lhsT=picked_words[hf][:, a, 2 * col : 2 * (col + P)].bitcast(FP4X4),
-                        lhsT_scale=picked_scales[:, a, jt * P : (jt + 1) * P],
-                        rhs=up_weights[m][:, a, :].bitcast(FP8X4),
+                        lhsT_scale=picked_scales[a][:, jt * P : (jt + 1) * P],
+                        rhs=up_weights[:, m, a, :].bitcast(FP8X4),
                         rhs_scale=weight_scales[:, m * PASSES + a, :],
                         start=(a == 0),
                         stop=(a == PASSES - 1),
                     )
                 sums.append(acc[:].rearrange("p (m u e) -> p u m e", u=2, e=2))
-            activated = ring.tile([P, 2, P, 2], F32, name="activated")
+            activated = ring.tile([P, 2, P, 2], F32, name="activated", tag="wide", bufs=4, align_bytes=64)
             nc.scalar.activation(activated[:], sums[0], GELU)
-            h = ring.tile([P, 2, P, 2], BF16, name="h", bufs=4)
+            h = ring.tile([P, 2, P, 2], BF16, name="h", bufs=5)
             nc.vector.tensor_tensor(h[:], sums[1], activated[:], MULT)
             return h
 
@@ -162,45 +162,55 @@ def tile_list_gmlpt_gelu_gateP_kernel(
                     )
                 nc.scalar.copy(y_rows[c][:, first : first + 2, :], y[:])
 
-        for c in range(CHUNKS):
+        def quantize_h(pair):
             grouped = ring.tile([P, CHUNK, 2], F32, name="grouped", align_bytes=64, bufs=2)
             codes = ring.tile([P, CHUNK], U32, name="h_codes", align_bytes=64, bufs=2)
             scales = ring.tile([P, CHUNK], U8, name="h_scales", align_bytes=64, bufs=2)
-            turn([first_stage(2 * c), first_stage(2 * c + 1)], grouped[:])
+            turn(pair, grouped[:])
             nc.vector.quantize_mx(
                 out=codes[:].bitcast(FP8X4),
                 scales=scales[:],
                 in_=grouped[:].rearrange("p j u -> p (j u)").bitcast(BF16),
             )
-            second_stage(c, codes, scales)
+            return codes, scales
 
+        h_tiles, quantized = [], []
+        for step in range(2 * CHUNKS + 3):
+            if step < 2 * CHUNKS:
+                h_tiles.append(first_stage(step))
+            if step >= 3 and step % 2 == 1:
+                c = (step - 3) // 2
+                quantized.append(quantize_h(h_tiles[2 * c : 2 * c + 2]))
+            if step >= 4 and step % 2 == 0:
+                c = (step - 4) // 2
+                second_stage(c, *quantized[c])
+
+        rounded = [
+            ring.tile([P, CHUNK, 4], BF16, name="rounded%d" % c, tag="wide", bufs=4, align_bytes=64) for c in range(CHUNKS)
+        ]
         out_rows = out_0.rearrange("(p t) j -> p t j", t=4)
-        for hf in range(HALVES):
-            nc.vector.tensor_copy(picked_gates[hf][:], gates[0][:].indirect(entries(hf * HALF, HALF)))
-        for c in range(CHUNKS):
-            cols = slice(c * CHUNK, (c + 1) * CHUNK)
-            hf, col = divmod(c * CHUNK, HALF)
-            nc.vector.tensor_tensor(early[:, 0, cols], picked_gates[hf][:, col : col + CHUNK], y_rows[c][:, 0, :], MULT)
-            nc.vector.tensor_tensor(early[:, 1, cols], gates[1][:].indirect(entries(c * CHUNK, CHUNK)), y_rows[c][:, 1, :], MULT)
-            nc.scalar.copy(rounded[c][:, :, 0:2], early[:, :, cols].rearrange("p t j -> p j t"))
-        nc.sync.dma_start(out_rows[:, 0:2, :], early[:])
-        for t in (2, 3):
-            for c in range(CHUNKS):
-                nc.vector.tensor_tensor(
-                    late[c][:, t - 2, :], gates[t][:].indirect(entries(c * CHUNK, CHUNK)), y_rows[c][:, t, :], MULT
-                )
         word_rows = out_1[0].rearrange("p j i -> p (j i)").bitcast(I32)
-        for c in range(CHUNKS):
+
+        def finish(c):
             cols = slice(c * CHUNK, (c + 1) * CHUNK)
-            hf, col = divmod(c * CHUNK, HALF)
-            nc.sync.dma_start(out_rows[:, 2:4, cols], late[c][:])
-            nc.scalar.copy(rounded[c][:, :, 2:4], late[c][:].rearrange("p t j -> p j t"))
+            rows = products[c][:, 2:4, :]
+            nc.sync.dma_start(out_rows[:, 2:4, cols], rows)
+            nc.scalar.copy(rounded[c][:, :, 2:4], rows.rearrange("p t j -> p j t"))
             nc.vector.quantize_mx(
-                out=out_codes[hf][:, col : col + CHUNK].bitcast(FP8X4),
+                out=out_codes[c][:].bitcast(FP8X4),
                 scales=out_scales[:, cols],
                 in_=rounded[c][:].rearrange("p j t -> p (j t)"),
             )
-            if col + CHUNK == HALF:
-                nc.sync.dma_start(word_rows[:, hf * HALF : (hf + 1) * HALF], out_codes[hf][:])
+            nc.sync.dma_start(word_rows[:, cols], out_codes[c][:])
+
+        for t in range(4):
+            for c in range(CHUNKS):
+                nc.vector.tensor_tensor(products[c][:, t, :], gates[t][:].indirect(entries(c * CHUNK, CHUNK)), y_rows[c][:, t, :], MULT)
+        for c in range(CHUNKS):
+            cols = slice(c * CHUNK, (c + 1) * CHUNK)
+            nc.scalar.copy(rounded[c][:, :, 0:2], products[c][:, 0:2, :].rearrange("p t j -> p j t"))
+            nc.sync.dma_start(out_rows[:, 0:2, cols], products[c][:, 0:2, :])
+        for c in range(CHUNKS):
+            finish(c)
         for q in range(4):
             nc.scalar.dma_start(out_2[0, 4 * q : 4 * q + 4, :].bitcast(I32), out_scales[32 * q : 32 * q + 4, :].bitcast(I32))

@@ -23,6 +23,10 @@ HALF = 512
 HALVES = J // HALF
 CHUNK = 256
 CHUNKS = J // CHUNK
+WG_AT = J
+WU_AT = WG_AT + R
+WD_AT = WU_AT + R
+PLANE = WD_AT + N // 2
 
 
 def tile_list_gmlpt_gelu_gateP_kernel(
@@ -41,33 +45,25 @@ def tile_list_gmlpt_gelu_gateP_kernel(
         def entries(start, count):
             return offsets[:, start // 16 : (start + count) // 16]
 
-        table = held.tile([P, T], I32, name="table", tag="slot1", align_bytes=64)
-        nc.gpsimd.dma_start(table[:], tab_words[0].rearrange("p t b -> p (t b)").bitcast(I32))
+        table_scales = held.tile([P, T], U8, name="table_scales")
+        nc.sync.dma_start(table_scales[96:128, :].bitcast(I32), tab_scales.rearrange("a q t -> q a t").bitcast(I32))
+        nc.vector.memset(table_scales[0:96, :].bitcast(I32), 0)
 
-        table_scales = reused.tile([P, T], U8, name="table_scales", offset=6144)
-        nc.sync.dma_start(table_scales[0:32, :].bitcast(I32), tab_scales.rearrange("a q t -> (a q) t").bitcast(I32))
-        nc.vector.memset(table_scales[32:64, :].bitcast(I32), 0)
-        nc.vector.memset(table_scales[64:128, :].bitcast(I32), 0)
+        staged = held.tile([P, PLANE], U8, name="staged", align_bytes=64)
+        nc.sync.dma_start(staged[96:128, WG_AT : WG_AT + R].bitcast(I32), wg_scales.rearrange("a q n -> q a n").bitcast(I32))
+        nc.sync.dma_start(staged[96:128, WU_AT : WU_AT + R].bitcast(I32), wu_scales.rearrange("a q n -> q a n").bitcast(I32))
+        nc.sync.dma_start(
+            staged[96:128, WD_AT:PLANE].bitcast(I32), wd_scales[0].rearrange("q (h n) -> (q h) n", h=2).bitcast(I32)
+        )
 
-        staged = held.tile([P, 2 * PASSES + 1, R], U8, name="staged")
-        for first, count, scales in ((0, PASSES, wg_scales), (PASSES, PASSES, wu_scales), (2 * PASSES, 1, wd_scales)):
-            nc.sync.dma_start(
-                staged[0:P:8, first : first + count, :].bitcast(I32), scales.rearrange("a q n -> q a n").bitcast(I32)
-            )
-        wd_raw = held.tile([P, N // 2], I32, name="wd_raw")
-        nc.sync.dma_start(wd_raw[:], wd_words[0].bitcast(I32))
-        wd = held.tile([P, 4, 2 * P], U8, name="wd", align_bytes=64)
-        nc.vector.tensor_copy(wd[:].bitcast(U16), wd_raw[:].bitcast(U16).rearrange("p (m t) -> p t m", t=4))
+        table = reused.tile([P, T], I32, name="table", offset=36864, align_bytes=64)
+        nc.sync.dma_start(table[:], tab_words[0].rearrange("p t b -> p (t b)").bitcast(I32))
 
-        weight_scales = held.tile([P, 2 * PASSES + 1, R], U8, name="weight_scales", align_bytes=64)
-        nc.vector.memset(weight_scales[:].bitcast(I32), 0)
-        picked_scales = [held.tile([P, J], U8, name="picked_scales%d" % a, align_bytes=64) for a in range(PASSES)]
-        for plane in picked_scales:
-            nc.vector.memset(plane[:].bitcast(I32), 0)
-        for q in range(4):
-            nc.scalar.dma_start(
-                weight_scales[32 * q : 32 * q + 4, :, :].bitcast(I32), staged[32 * q : 32 * q + 32 : 8, :, :].bitcast(I32)
-            )
+        wg = held.tile([P, PASSES, R], I32, name="wg", align_bytes=64)
+        nc.sync.dma_start(wg[:], wg_words.rearrange("a p r i -> p a (r i)").bitcast(I32))
+
+        planes = held.tile([P, PASSES, PLANE], U8, name="planes", align_bytes=64)
+        nc.vector.memset(planes[:].bitcast(I32), 0)
 
         identity = held.tile([P, P], F32, name="identity")
         make_identity(nc, identity[:])
@@ -76,26 +72,23 @@ def tile_list_gmlpt_gelu_gateP_kernel(
         nc.vector.memset(warm[:, 0:4], 0.0)
         nc.scalar.activation(warm[:, 4:8], warm[:, 0:4], GELU)
 
-        picked_rows = held.tile([P, J], U8, name="picked_rows", tag="slot3", align_bytes=64)
+        picked_rows = reused.tile([P, J], U8, name="picked_rows", offset=7680, align_bytes=64)
         nc.vector.tensor_copy(picked_rows[:], table_scales[:].indirect(offsets[:]))
+        nc.vector.tensor_copy(staged[:, 0:J].bitcast(I32), picked_rows[:].bitcast(I32))
+        for q in range(4):
+            nc.sync.dma_start(planes[32 * q : 32 * q + 4, :, :].bitcast(I32), staged[96 + 8 * q : 104 + 8 * q, :].bitcast(I32))
 
-        def move_scale_rows(a, q):
-            row = 16 * a + 4 * q
-            nc.sync.dma_start(picked_scales[a][32 * q : 32 * q + 4, :].bitcast(I32), picked_rows[row : row + 4, :].bitcast(I32))
-
-        moves = [(a, q) for a in range(PASSES) for q in range(4)]
-        for a, q in moves[:6]:
-            move_scale_rows(a, q)
-        up_weights = reused.tile([P, 2, PASSES, R], I32, name="up_weights", offset=0, align_bytes=64)
-        for m, words in enumerate((wg_words, wu_words)):
-            nc.sync.dma_start(up_weights[:, m, :, :], words.rearrange("a p r i -> p a (r i)").bitcast(I32))
-        for a, q in moves[6:]:
-            move_scale_rows(a, q)
+        late = reused.tile([P, PASSES * R + N // 2], I32, name="late", offset=3072, align_bytes=64)
+        wu = late[:, 0 : PASSES * R].rearrange("p (a r) -> p a r", a=PASSES)
+        wd_raw = late[:, PASSES * R :]
+        nc.sync.dma_start(wu, wu_words.rearrange("a p r i -> p a (r i)").bitcast(I32))
+        nc.sync.dma_start(wd_raw, wd_words[0].bitcast(I32))
+        up_weights = (wg[:], wu)
 
         picked_words = []
         for hf in range(HALVES):
             listed = entries(hf * HALF, HALF)
-            pairs = held.tile([P, HALF], U32, name="picked_pairs%d" % hf, tag="slot2", align_bytes=64)
+            pairs = reused.tile([P, HALF], U32, name="picked_pairs%d" % hf, offset=65536, align_bytes=64)
             nc.vector.tensor_copy(pairs[:], table[:].bitcast(U32).indirect(listed))
             words = held.tile([P, PASSES, 2 * HALF], U8, name="picked_words%d" % hf, align_bytes=64)
             nc.vector.tensor_copy(
@@ -104,16 +97,21 @@ def tile_list_gmlpt_gelu_gateP_kernel(
             picked_words.append(words)
 
         gate_rows = gT.rearrange("(p t) c -> t p c", t=4)
-        gates = [reused.tile([P, T], F32, name="gate0", offset=8192)]
-        gates.extend(held.tile([P, T], F32, name="gate%d" % t, tag="slot%d" % t, align_bytes=64) for t in range(1, 4))
+        gates = [
+            reused.tile([P, T], F32, name="gate%d" % t, offset=at, align_bytes=64)
+            for t, at in enumerate((8192, 24576, 49152, 65536))
+        ]
         for t in range(4):
             nc.sync.dma_start(gates[t][:], gate_rows[t])
-
+        wd = held.tile([P, 4, 2 * P], U8, name="wd", align_bytes=64)
+        nc.vector.tensor_copy(wd[:].bitcast(U16), wd_raw.bitcast(U16).rearrange("p (m t) -> p t m", t=4))
         wd_scale = held.tile([P, 4, P], U8, name="wd_scale", align_bytes=64)
-        nc.vector.tensor_copy(wd_scale[:], weight_scales[:, 2 * PASSES, :].rearrange("p (m t) -> p t m", t=4))
+        nc.vector.tensor_copy(
+            wd_scale[:].rearrange("p t (h m) -> p t h m", h=2),
+            planes[:, :, WD_AT:PLANE].rearrange("p h (m t) -> p t h m", t=4),
+        )
 
         y_rows = [held.tile([P, 4, CHUNK], F32, name="y_rows%d" % c) for c in range(CHUNKS)]
-        products = [held.tile([P, 4, CHUNK], F32, name="products%d" % c) for c in range(CHUNKS)]
         out_codes = [held.tile([P, CHUNK], I32, name="out_codes%d" % c, align_bytes=64) for c in range(CHUNKS)]
         out_scales = held.tile([P, J], U8, name="out_scales", align_bytes=64)
 
@@ -126,9 +124,9 @@ def tile_list_gmlpt_gelu_gateP_kernel(
                     nc.tensor.matmul_mx(
                         out=acc[:],
                         lhsT=picked_words[hf][:, a, 2 * col : 2 * (col + P)].bitcast(FP4X4),
-                        lhsT_scale=picked_scales[a][:, jt * P : (jt + 1) * P],
-                        rhs=up_weights[:, m, a, :].bitcast(FP8X4),
-                        rhs_scale=weight_scales[:, m * PASSES + a, :],
+                        lhsT_scale=planes[:, a, jt * P : (jt + 1) * P],
+                        rhs=up_weights[m][:, a, :].bitcast(FP8X4),
+                        rhs_scale=planes[:, a, WG_AT + m * R : WG_AT + (m + 1) * R],
                         start=(a == 0),
                         stop=(a == PASSES - 1),
                     )
@@ -147,9 +145,13 @@ def tile_list_gmlpt_gelu_gateP_kernel(
                     nc.tensor.transpose(turned[:, i, u, :], words[:, u * P : (u + 1) * P], identity[:])
             nc.scalar.copy(grouped.rearrange("p (i j) u -> p i j u", i=2), turned[:].rearrange("p i u j -> p i j u"))
 
-        def second_stage(c, codes, scales):
-            for first in (0, 2):
-                y = psum.tile([P, 2, CHUNK], F32, name="y", bufs=2)
+        def second_stage(c, first):
+            codes, scales = quantized[c]
+            if True:
+                if first == 2 and c < 3:
+                    y = psum.tile([P, 2, CHUNK], F32, name="y_late", tag="sum1", bufs=3)
+                else:
+                    y = psum.tile([P, 2, CHUNK], F32, name="y", bufs=2)
                 for i in range(2):
                     nc.tensor.matmul_mx(
                         out=y[:, i, :],
@@ -162,10 +164,10 @@ def tile_list_gmlpt_gelu_gateP_kernel(
                     )
                 nc.scalar.copy(y_rows[c][:, first : first + 2, :], y[:])
 
-        def quantize_h(pair):
-            grouped = ring.tile([P, CHUNK, 2], F32, name="grouped", align_bytes=64, bufs=2)
-            codes = ring.tile([P, CHUNK], U32, name="h_codes", align_bytes=64, bufs=2)
-            scales = ring.tile([P, CHUNK], U8, name="h_scales", align_bytes=64, bufs=2)
+        def quantize_h(c, pair):
+            grouped = held.tile([P, CHUNK, 2], F32, name="grouped%d" % c, tag="chunk2" if c == 3 else "grouped%d" % c, align_bytes=64)
+            codes = ring.tile([P, CHUNK], U32, name="h_codes", align_bytes=64, bufs=4)
+            scales = ring.tile([P, CHUNK], U8, name="h_scales", align_bytes=64, bufs=4)
             turn(pair, grouped[:])
             nc.vector.quantize_mx(
                 out=codes[:].bitcast(FP8X4),
@@ -180,37 +182,43 @@ def tile_list_gmlpt_gelu_gateP_kernel(
                 h_tiles.append(first_stage(step))
             if step >= 3 and step % 2 == 1:
                 c = (step - 3) // 2
-                quantized.append(quantize_h(h_tiles[2 * c : 2 * c + 2]))
+                quantized.append(quantize_h(c, h_tiles[2 * c : 2 * c + 2]))
             if step >= 4 and step % 2 == 0:
                 c = (step - 4) // 2
-                second_stage(c, *quantized[c])
+                second_stage(c, 0)
 
+        early = held.tile([P, HALF], F32, name="early")
+        nc.vector.tensor_copy(early[:], gates[0][:].indirect(entries(HALF, HALF)))
+        for c in range(CHUNKS):
+            second_stage(c, 2)
+
+        products = [held.tile([P, 4, CHUNK], F32, name="products%d" % c, tag="chunk%d" % c, align_bytes=64) for c in range(CHUNKS)]
         rounded = [
             ring.tile([P, CHUNK, 4], BF16, name="rounded%d" % c, tag="wide", bufs=4, align_bytes=64) for c in range(CHUNKS)
         ]
         out_rows = out_0.rearrange("(p t) j -> p t j", t=4)
         word_rows = out_1[0].rearrange("p j i -> p (j i)").bitcast(I32)
 
-        def finish(c):
+        def gated(t, c):
+            if t == 0 and c >= 2:
+                gate = early[:, (c - 2) * CHUNK : (c - 1) * CHUNK]
+            else:
+                gate = gates[t][:].indirect(entries(c * CHUNK, CHUNK))
+            nc.vector.tensor_tensor(products[c][:, t, :], gate, y_rows[c][:, t, :], MULT)
+
+        for c in range(CHUNKS):
             cols = slice(c * CHUNK, (c + 1) * CHUNK)
-            rows = products[c][:, 2:4, :]
-            nc.sync.dma_start(out_rows[:, 2:4, cols], rows)
-            nc.scalar.copy(rounded[c][:, :, 2:4], rows.rearrange("p t j -> p j t"))
+            for first in (0, 2):
+                gated(first, c)
+                gated(first + 1, c)
+                rows = products[c][:, first : first + 2, :]
+                nc.scalar.copy(rounded[c][:, :, first : first + 2], rows.rearrange("p t j -> p j t"))
+                nc.sync.dma_start(out_rows[:, first : first + 2, cols], rows)
             nc.vector.quantize_mx(
                 out=out_codes[c][:].bitcast(FP8X4),
                 scales=out_scales[:, cols],
                 in_=rounded[c][:].rearrange("p j t -> p (j t)"),
             )
             nc.sync.dma_start(word_rows[:, cols], out_codes[c][:])
-
-        for t in range(4):
-            for c in range(CHUNKS):
-                nc.vector.tensor_tensor(products[c][:, t, :], gates[t][:].indirect(entries(c * CHUNK, CHUNK)), y_rows[c][:, t, :], MULT)
-        for c in range(CHUNKS):
-            cols = slice(c * CHUNK, (c + 1) * CHUNK)
-            nc.scalar.copy(rounded[c][:, :, 0:2], products[c][:, 0:2, :].rearrange("p t j -> p j t"))
-            nc.sync.dma_start(out_rows[:, 0:2, cols], products[c][:, 0:2, :])
-        for c in range(CHUNKS):
-            finish(c)
         for q in range(4):
             nc.scalar.dma_start(out_2[0, 4 * q : 4 * q + 4, :].bitcast(I32), out_scales[32 * q : 32 * q + 4, :].bitcast(I32))

@@ -27,6 +27,7 @@ WG_AT = J
 WU_AT = WG_AT + R
 WD_AT = WU_AT + R
 PLANE = WD_AT + N // 2
+LAST_AT = 90112
 
 
 def tile_list_gmlpt_gelu_gateP_kernel(
@@ -59,6 +60,8 @@ def tile_list_gmlpt_gelu_gateP_kernel(
         table = reused.tile([P, T], I32, name="table", offset=36864, align_bytes=64)
         nc.sync.dma_start(table[:], tab_words[0].rearrange("p t b -> p (t b)").bitcast(I32))
 
+        wd_raw = held.tile([P, N // 2], I32, name="wd_raw", align_bytes=64)
+        nc.sync.dma_start(wd_raw[:], wd_words[0].bitcast(I32))
         wg = held.tile([P, PASSES, R], I32, name="wg", align_bytes=64)
         nc.sync.dma_start(wg[:], wg_words.rearrange("a p r i -> p a (r i)").bitcast(I32))
 
@@ -75,25 +78,34 @@ def tile_list_gmlpt_gelu_gateP_kernel(
         picked_rows = reused.tile([P, J], U8, name="picked_rows", offset=7680, align_bytes=64)
         nc.vector.tensor_copy(picked_rows[:], table_scales[:].indirect(offsets[:]))
         nc.vector.tensor_copy(staged[:, 0:J].bitcast(I32), picked_rows[:].bitcast(I32))
-        for q in range(4):
+        for q in (0, 2, 1, 3):
             nc.sync.dma_start(planes[32 * q : 32 * q + 4, :, :].bitcast(I32), staged[96 + 8 * q : 104 + 8 * q, :].bitcast(I32))
 
-        late = reused.tile([P, PASSES * R + N // 2], I32, name="late", offset=3072, align_bytes=64)
-        wu = late[:, 0 : PASSES * R].rearrange("p (a r) -> p a r", a=PASSES)
-        wd_raw = late[:, PASSES * R :]
-        nc.sync.dma_start(wu, wu_words.rearrange("a p r i -> p a (r i)").bitcast(I32))
-        nc.sync.dma_start(wd_raw, wd_words[0].bitcast(I32))
-        up_weights = (wg[:], wu)
+        wu = reused.tile([P, PASSES, R], I32, name="wu", offset=4096, align_bytes=64)
+        nc.sync.dma_start(wu[:], wu_words.rearrange("a p r i -> p a (r i)").bitcast(I32))
+        up_weights = (wg, wu)
+
+        idle = psum.tile([P, R], F32, name="idle", tag="y", bufs=2)
+        for repeat in range(2):
+            nc.tensor.matmul_mx(
+                out=idle[:],
+                lhsT=wd_raw[:, 0 : P // 2].bitcast(FP4X4),
+                lhsT_scale=staged[:, 0:P],
+                rhs=wg[:, 0, :].bitcast(FP8X4),
+                rhs_scale=staged[:, 0:R],
+                start=True,
+                stop=True,
+            )
 
         picked_words = []
         for hf in range(HALVES):
             listed = entries(hf * HALF, HALF)
-            pairs = reused.tile([P, HALF], U32, name="picked_pairs%d" % hf, offset=65536, align_bytes=64)
+            pairs = reused.tile([P, HALF], U32, name="picked_pairs%d" % hf, offset=81920 - 1024, align_bytes=64)
             nc.vector.tensor_copy(pairs[:], table[:].bitcast(U32).indirect(listed))
             words = held.tile([P, PASSES, 2 * HALF], U8, name="picked_words%d" % hf, align_bytes=64)
-            nc.vector.tensor_copy(
-                words[:].bitcast(U16), pairs[:].bitcast(U16).rearrange("p (j a) -> p a j", a=PASSES)
-            )
+            parted = pairs[:].bitcast(U16).rearrange("p (j a) -> p a j", a=PASSES)
+            for lo, hi in ((0, P), (P, HALF)) if hf == 0 else ((0, HALF),):
+                nc.vector.tensor_copy(words[:].bitcast(U16)[:, :, lo:hi], parted[:, :, lo:hi])
             picked_words.append(words)
 
         gate_rows = gT.rearrange("(p t) c -> t p c", t=4)
@@ -103,8 +115,8 @@ def tile_list_gmlpt_gelu_gateP_kernel(
         ]
         for t in range(4):
             nc.sync.dma_start(gates[t][:], gate_rows[t])
-        wd = held.tile([P, 4, 2 * P], U8, name="wd", align_bytes=64)
-        nc.vector.tensor_copy(wd[:].bitcast(U16), wd_raw.bitcast(U16).rearrange("p (m t) -> p t m", t=4))
+        wd = reused.tile([P, 4, 2 * P], U8, name="wd", offset=81920, align_bytes=64)
+        nc.vector.tensor_copy(wd[:].bitcast(U16), wd_raw[:].bitcast(U16).rearrange("p (m t) -> p t m", t=4))
         wd_scale = held.tile([P, 4, P], U8, name="wd_scale", align_bytes=64)
         nc.vector.tensor_copy(
             wd_scale[:].rearrange("p t (h m) -> p t h m", h=2),
@@ -112,7 +124,7 @@ def tile_list_gmlpt_gelu_gateP_kernel(
         )
 
         y_rows = [held.tile([P, 4, CHUNK], F32, name="y_rows%d" % c) for c in range(CHUNKS)]
-        out_codes = [held.tile([P, CHUNK], I32, name="out_codes%d" % c, align_bytes=64) for c in range(CHUNKS)]
+        out_codes = held.tile([P, J], I32, name="out_codes", align_bytes=64)
         out_scales = held.tile([P, J], U8, name="out_scales", align_bytes=64)
 
         def first_stage(jt):
@@ -131,7 +143,10 @@ def tile_list_gmlpt_gelu_gateP_kernel(
                         stop=(a == PASSES - 1),
                     )
                 sums.append(acc[:].rearrange("p (m u e) -> p u m e", u=2, e=2))
-            activated = ring.tile([P, 2, P, 2], F32, name="activated", tag="wide", bufs=4, align_bytes=64)
+            if jt >= 6:
+                activated = held.tile([P, 2, P, 2], F32, name="activated%d" % jt, tag=("round0", "low1")[jt - 6], align_bytes=64)
+            else:
+                activated = ring.tile([P, 2, P, 2], F32, name="activated", bufs=4, align_bytes=64)
             nc.scalar.activation(activated[:], sums[0], GELU)
             h = ring.tile([P, 2, P, 2], BF16, name="h", bufs=5)
             nc.vector.tensor_tensor(h[:], sums[1], activated[:], MULT)
@@ -162,10 +177,16 @@ def tile_list_gmlpt_gelu_gateP_kernel(
                         start=True,
                         stop=True,
                     )
-                nc.scalar.copy(y_rows[c][:, first : first + 2, :], y[:])
+                if first == 0 and c >= 2:
+                    kept[c] = y
+                else:
+                    nc.scalar.copy(y_rows[c][:, first : first + 2, :], y[:])
 
         def quantize_h(c, pair):
-            grouped = held.tile([P, CHUNK, 2], F32, name="grouped%d" % c, tag="chunk2" if c == 3 else "grouped%d" % c, align_bytes=64)
+            if c == 3:
+                grouped = reused.tile([P, CHUNK, 2], F32, name="grouped3", offset=LAST_AT - 1024, align_bytes=64)
+            else:
+                grouped = held.tile([P, CHUNK, 2], F32, name="grouped%d" % c, align_bytes=64)
             codes = ring.tile([P, CHUNK], U32, name="h_codes", align_bytes=64, bufs=4)
             scales = ring.tile([P, CHUNK], U8, name="h_scales", align_bytes=64, bufs=4)
             turn(pair, grouped[:])
@@ -176,7 +197,7 @@ def tile_list_gmlpt_gelu_gateP_kernel(
             )
             return codes, scales
 
-        h_tiles, quantized = [], []
+        h_tiles, quantized, kept = [], [], [None] * CHUNKS
         for step in range(2 * CHUNKS + 3):
             if step < 2 * CHUNKS:
                 h_tiles.append(first_stage(step))
@@ -187,38 +208,55 @@ def tile_list_gmlpt_gelu_gateP_kernel(
                 c = (step - 4) // 2
                 second_stage(c, 0)
 
-        early = held.tile([P, HALF], F32, name="early")
-        nc.vector.tensor_copy(early[:], gates[0][:].indirect(entries(HALF, HALF)))
-        for c in range(CHUNKS):
+        early = held.tile([P, 2, HALF], F32, name="early")
+        for t in range(2):
+            nc.vector.tensor_copy(early[:, t, :], gates[t][:].indirect(entries(HALF, HALF)))
+        for c in range(CHUNKS - 1):
             second_stage(c, 2)
 
-        products = [held.tile([P, 4, CHUNK], F32, name="products%d" % c, tag="chunk%d" % c, align_bytes=64) for c in range(CHUNKS)]
+        late = reused.tile([P, 2 * J + 2 * CHUNK], F32, name="late", offset=LAST_AT, align_bytes=64)
+        high = late[:, 0 : 2 * J].rearrange("p (t j) -> p t j", t=2)
+        low = [
+            late[:, 2 * J :].rearrange("p (t j) -> p t j", t=2) if c == 2 else held.tile([P, 2, CHUNK], F32, name="low%d" % c, tag="low%d" % c, align_bytes=64)[:]
+            for c in range(CHUNKS)
+        ]
+        middle = reused.tile([P, 2, CHUNK, 4], BF16, name="middle", offset=LAST_AT - 4096, align_bytes=64)
         rounded = [
-            ring.tile([P, CHUNK, 4], BF16, name="rounded%d" % c, tag="wide", bufs=4, align_bytes=64) for c in range(CHUNKS)
+            middle[:, c - 1, :, :] if c in (1, 2) else held.tile([P, CHUNK, 4], BF16, name="rounded%d" % c, tag="round%d" % c, align_bytes=64)[:]
+            for c in range(CHUNKS)
         ]
         out_rows = out_0.rearrange("(p t) j -> p t j", t=4)
         word_rows = out_1[0].rearrange("p j i -> p (j i)").bitcast(I32)
 
-        def gated(t, c):
-            if t == 0 and c >= 2:
-                gate = early[:, (c - 2) * CHUNK : (c - 1) * CHUNK]
-            else:
-                gate = gates[t][:].indirect(entries(c * CHUNK, CHUNK))
-            nc.vector.tensor_tensor(products[c][:, t, :], gate, y_rows[c][:, t, :], MULT)
+        def gated(t, c, product):
+            gate = gates[t][:].indirect(entries(c * CHUNK, CHUNK))
+            nc.vector.tensor_tensor(product, gate, y_rows[c][:, t, :], MULT)
 
         for c in range(CHUNKS):
             cols = slice(c * CHUNK, (c + 1) * CHUNK)
-            for first in (0, 2):
-                gated(first, c)
-                gated(first + 1, c)
-                rows = products[c][:, first : first + 2, :]
-                nc.scalar.copy(rounded[c][:, :, first : first + 2], rows.rearrange("p t j -> p j t"))
-                nc.sync.dma_start(out_rows[:, first : first + 2, cols], rows)
+            if c == CHUNKS - 1:
+                second_stage(c, 2)
+            if c >= 2:
+                nc.vector.tensor_tensor(low[c], kept[c][:], early[:, :, (c - 2) * CHUNK : (c - 1) * CHUNK], MULT)
+            else:
+                gated(0, c, low[c][:, 0, :])
+                gated(1, c, low[c][:, 1, :])
+            nc.scalar.copy(rounded[c][:, :, 0:2], low[c].rearrange("p t j -> p j t"))
+            nc.sync.dma_start(out_rows[:, 0:2, cols], low[c])
+            gated(2, c, high[:, 0, cols])
+        nc.sync.dma_start(out_rows[:, 2, :], high[:, 0, :])
+        for c in range(CHUNKS):
+            cols = slice(c * CHUNK, (c + 1) * CHUNK)
+            gated(3, c, high[:, 1, cols])
+            nc.scalar.copy(rounded[c][:, :, 2:4], high[:, :, cols].rearrange("p t j -> p j t"))
             nc.vector.quantize_mx(
-                out=out_codes[c][:].bitcast(FP8X4),
+                out=out_codes[:, cols].bitcast(FP8X4),
                 scales=out_scales[:, cols],
-                in_=rounded[c][:].rearrange("p j t -> p (j t)"),
+                in_=rounded[c].rearrange("p j t -> p (j t)"),
             )
-            nc.sync.dma_start(word_rows[:, cols], out_codes[c][:])
+            if c % 2 == 1:
+                half = slice((c - 1) * CHUNK, (c + 1) * CHUNK)
+                nc.sync.dma_start(out_rows[:, 3, half], high[:, 1, half])
+                nc.sync.dma_start(word_rows[:, half], out_codes[:, half])
         for q in range(4):
             nc.scalar.dma_start(out_2[0, 4 * q : 4 * q + 4, :].bitcast(I32), out_scales[32 * q : 32 * q + 4, :].bitcast(I32))

@@ -62,8 +62,8 @@ def tile_list_gmlpt_gelu_gateP_kernel(
 
         wd_raw = held.tile([P, N // 2], I32, name="wd_raw", align_bytes=64)
         nc.sync.dma_start(wd_raw[:], wd_words[0].bitcast(I32))
-        wg = held.tile([P, PASSES, R], I32, name="wg", align_bytes=64)
-        nc.sync.dma_start(wg[:], wg_words.rearrange("a p r i -> p a (r i)").bitcast(I32))
+        wg_first = held.tile([P, R], I32, name="wg_first", align_bytes=64)
+        nc.sync.dma_start(wg_first[:], wg_words[0].rearrange("p r i -> p (r i)").bitcast(I32))
 
         planes = held.tile([P, PASSES, PLANE], U8, name="planes", align_bytes=64)
         nc.vector.memset(planes[:].bitcast(I32), 0)
@@ -71,9 +71,6 @@ def tile_list_gmlpt_gelu_gateP_kernel(
         identity = held.tile([P, P], F32, name="identity")
         make_identity(nc, identity[:])
 
-        warm = held.tile([P, 8], F32, name="warm")
-        nc.vector.memset(warm[:, 0:4], 0.0)
-        nc.scalar.activation(warm[:, 4:8], warm[:, 0:4], GELU)
 
         picked_rows = reused.tile([P, J], U8, name="picked_rows", offset=7680, align_bytes=64)
         nc.vector.tensor_copy(picked_rows[:], table_scales[:].indirect(offsets[:]))
@@ -81,9 +78,10 @@ def tile_list_gmlpt_gelu_gateP_kernel(
         for q in (0, 2, 1, 3):
             nc.sync.dma_start(planes[32 * q : 32 * q + 4, :, :].bitcast(I32), staged[96 + 8 * q : 104 + 8 * q, :].bitcast(I32))
 
-        wu = reused.tile([P, PASSES, R], I32, name="wu", offset=4096, align_bytes=64)
-        nc.sync.dma_start(wu[:], wu_words.rearrange("a p r i -> p a (r i)").bitcast(I32))
-        up_weights = (wg, wu)
+        rest = reused.tile([P, 1 + PASSES, R], I32, name="rest", offset=2048, align_bytes=64)
+        nc.sync.dma_start(rest[:, 0, :], wg_words[1].rearrange("p r i -> p (r i)").bitcast(I32))
+        nc.sync.dma_start(rest[:, 1:, :], wu_words.rearrange("a p r i -> p a (r i)").bitcast(I32))
+        up_weights = ((wg_first[:], rest[:, 0, :]), (rest[:, 1, :], rest[:, 2, :]))
 
         idle = psum.tile([P, R], F32, name="idle", tag="y", bufs=2)
         for repeat in range(2):
@@ -91,7 +89,7 @@ def tile_list_gmlpt_gelu_gateP_kernel(
                 out=idle[:],
                 lhsT=wd_raw[:, 0 : P // 2].bitcast(FP4X4),
                 lhsT_scale=staged[:, 0:P],
-                rhs=wg[:, 0, :].bitcast(FP8X4),
+                rhs=wg_first[:].bitcast(FP8X4),
                 rhs_scale=staged[:, 0:R],
                 start=True,
                 stop=True,
@@ -137,7 +135,7 @@ def tile_list_gmlpt_gelu_gateP_kernel(
                         out=acc[:],
                         lhsT=picked_words[hf][:, a, 2 * col : 2 * (col + P)].bitcast(FP4X4),
                         lhsT_scale=planes[:, a, jt * P : (jt + 1) * P],
-                        rhs=up_weights[m][:, a, :].bitcast(FP8X4),
+                        rhs=up_weights[m][a].bitcast(FP8X4),
                         rhs_scale=planes[:, a, WG_AT + m * R : WG_AT + (m + 1) * R],
                         start=(a == 0),
                         stop=(a == PASSES - 1),
@@ -257,6 +255,8 @@ def tile_list_gmlpt_gelu_gateP_kernel(
             if c % 2 == 1:
                 half = slice((c - 1) * CHUNK, (c + 1) * CHUNK)
                 nc.sync.dma_start(out_rows[:, 3, half], high[:, 1, half])
-                nc.sync.dma_start(word_rows[:, half], out_codes[:, half])
-        for q in range(4):
+            if c >= 1:
+                done = slice(0, HALF) if c == 1 else cols
+                nc.sync.dma_start(word_rows[:, done], out_codes[:, done])
+        for q in (0, 2, 1, 3):
             nc.scalar.dma_start(out_2[0, 4 * q : 4 * q + 4, :].bitcast(I32), out_scales[32 * q : 32 * q + 4, :].bitcast(I32))

@@ -19,15 +19,26 @@ GELU = mybir.ActivationFunctionType.Gelu_apprx_tanh
 
 P = 128
 PASSES = K // 512
-HALF = 512
-HALVES = J // HALF
+HALF = J // 2
 CHUNK = 256
 CHUNKS = J // CHUNK
+
 WG_AT = J
 WU_AT = WG_AT + R
 WD_AT = WU_AT + R
-PLANE = WD_AT + N // 2
-LAST_AT = 90112
+PLANES = WD_AT + N // 2
+ROWS_AT = 96
+QUADRANTS = (0, 2, 1, 3)
+
+GATE_BYTES = 4 * T
+OVERLAP = 4096
+GATE0_AT = 8192
+GATE1_AT = GATE0_AT + GATE_BYTES
+TABLE_AT = GATE1_AT + GATE_BYTES - OVERLAP
+GATE2_AT = TABLE_AT + GATE_BYTES - OVERLAP
+GATE3_AT = GATE2_AT + GATE_BYTES
+GATES_END = GATE3_AT + GATE_BYTES
+LATE_AT = GATES_END + 8192
 
 
 def tile_list_gmlpt_gelu_gateP_kernel(
@@ -36,9 +47,9 @@ def tile_list_gmlpt_gelu_gateP_kernel(
     nc = tc.nc
     with ExitStack() as ctx:
         held = ctx.enter_context(tc.tile_pool(name="held", bufs=1))
-        reused = ctx.enter_context(tc.tile_pool(name="reused", bufs=1))
-        ring = ctx.enter_context(tc.tile_pool(name="ring", bufs=3))
-        psum = ctx.enter_context(tc.psum_pool(name="psum", bufs=2))
+        shared = ctx.enter_context(tc.tile_pool(name="shared", bufs=1))
+        ring = ctx.enter_context(tc.tile_pool(name="ring", bufs=1))
+        psum = ctx.enter_context(tc.psum_pool(name="psum", bufs=1))
 
         offsets = held.tile([P, J // 16], U16, name="offsets")
         nc.sync.dma_start(offsets[:], offs)
@@ -46,47 +57,46 @@ def tile_list_gmlpt_gelu_gateP_kernel(
         def entries(start, count):
             return offsets[:, start // 16 : (start + count) // 16]
 
-        table_scales = held.tile([P, T], U8, name="table_scales")
-        nc.sync.dma_start(table_scales[96:128, :].bitcast(I32), tab_scales.rearrange("a q t -> q a t").bitcast(I32))
-        nc.vector.memset(table_scales[0:96, :].bitcast(I32), 0)
+        def chunk(c):
+            return slice(c * CHUNK, (c + 1) * CHUNK)
 
-        staged = held.tile([P, PLANE], U8, name="staged", align_bytes=64)
-        nc.sync.dma_start(staged[96:128, WG_AT : WG_AT + R].bitcast(I32), wg_scales.rearrange("a q n -> q a n").bitcast(I32))
-        nc.sync.dma_start(staged[96:128, WU_AT : WU_AT + R].bitcast(I32), wu_scales.rearrange("a q n -> q a n").bitcast(I32))
-        nc.sync.dma_start(
-            staged[96:128, WD_AT:PLANE].bitcast(I32), wd_scales[0].rearrange("q (h n) -> (q h) n", h=2).bitcast(I32)
-        )
-
-        table = reused.tile([P, T], I32, name="table", offset=36864, align_bytes=64)
-        nc.sync.dma_start(table[:], tab_words[0].rearrange("p t b -> p (t b)").bitcast(I32))
+        rows = slice(ROWS_AT, P)
+        table_scales = held.tile([P, T], U8, name="table_scales", tag="window", align_bytes=64)
+        nc.sync.dma_start(table_scales[rows, :].bitcast(I32), tab_scales.rearrange("a b t -> b a t").bitcast(I32))
+        nc.vector.memset(table_scales[0:ROWS_AT, :].bitcast(I32), 0)
+        staged = held.tile([P, PLANES], U8, name="staged", align_bytes=64)
+        nc.sync.dma_start(staged[rows, WG_AT:WU_AT].bitcast(I32), wg_scales.rearrange("a b r -> b a r").bitcast(I32))
+        nc.sync.dma_start(staged[rows, WU_AT:WD_AT].bitcast(I32), wu_scales.rearrange("a b r -> b a r").bitcast(I32))
+        nc.sync.dma_start(staged[rows, WD_AT:PLANES].bitcast(I32), wd_scales[0].rearrange("b (h n) -> (b h) n", h=2).bitcast(I32))
 
         wd_raw = held.tile([P, N // 2], I32, name="wd_raw", align_bytes=64)
         nc.sync.dma_start(wd_raw[:], wd_words[0].bitcast(I32))
+        table = shared.tile([P, T], I32, name="table", offset=TABLE_AT, align_bytes=64)
+        nc.sync.dma_start(table[:], tab_words[0].rearrange("p t b -> p (t b)").bitcast(I32))
         wg_first = held.tile([P, R], I32, name="wg_first", align_bytes=64)
         nc.sync.dma_start(wg_first[:], wg_words[0].rearrange("p r i -> p (r i)").bitcast(I32))
 
-        planes = held.tile([P, PASSES, PLANE], U8, name="planes", align_bytes=64)
+        planes = held.tile([P, PASSES, PLANES], U8, name="planes", align_bytes=64)
         nc.vector.memset(planes[:].bitcast(I32), 0)
-
         identity = held.tile([P, P], F32, name="identity")
         make_identity(nc, identity[:])
 
-
-        picked_rows = reused.tile([P, J], U8, name="picked_rows", offset=7680, align_bytes=64)
+        picked_rows = shared.tile([P, J], U8, name="picked_rows", offset=GATE0_AT - J // 2, align_bytes=64)
         nc.vector.tensor_copy(picked_rows[:], table_scales[:].indirect(offsets[:]))
         nc.vector.tensor_copy(staged[:, 0:J].bitcast(I32), picked_rows[:].bitcast(I32))
-        for q in (0, 2, 1, 3):
-            nc.sync.dma_start(planes[32 * q : 32 * q + 4, :, :].bitcast(I32), staged[96 + 8 * q : 104 + 8 * q, :].bitcast(I32))
+        for q in QUADRANTS:
+            first = ROWS_AT + 8 * q
+            nc.sync.dma_start(planes[32 * q : 32 * q + 4, :, :].bitcast(I32), staged[first : first + 8, :].bitcast(I32))
 
-        rest = reused.tile([P, 1 + PASSES, R], I32, name="rest", offset=2048, align_bytes=64)
-        nc.sync.dma_start(rest[:, 0, :], wg_words[1].rearrange("p r i -> p (r i)").bitcast(I32))
-        nc.sync.dma_start(rest[:, 1:, :], wu_words.rearrange("a p r i -> p a (r i)").bitcast(I32))
-        up_weights = ((wg_first[:], rest[:, 0, :]), (rest[:, 1, :], rest[:, 2, :]))
+        later = shared.tile([P, 1 + PASSES, R], I32, name="later", offset=GATE0_AT - (1 + PASSES) * 4 * R, align_bytes=64)
+        nc.sync.dma_start(later[:, 0, :], wg_words[1].rearrange("p r i -> p (r i)").bitcast(I32))
+        nc.sync.dma_start(later[:, 1:, :], wu_words.rearrange("a p r i -> p a (r i)").bitcast(I32))
+        up_weights = ((wg_first[:], later[:, 0, :]), (later[:, 1, :], later[:, 2, :]))
 
-        idle = psum.tile([P, R], F32, name="idle", tag="y", bufs=2)
+        unread = psum.tile([P, R], F32, name="unread", tag="y", bufs=2)
         for repeat in range(2):
             nc.tensor.matmul_mx(
-                out=idle[:],
+                out=unread[:],
                 lhsT=wd_raw[:, 0 : P // 2].bitcast(FP4X4),
                 lhsT_scale=staged[:, 0:P],
                 rhs=wg_first[:].bitcast(FP8X4),
@@ -96,44 +106,53 @@ def tile_list_gmlpt_gelu_gateP_kernel(
             )
 
         picked_words = []
-        for hf in range(HALVES):
-            listed = entries(hf * HALF, HALF)
-            pairs = reused.tile([P, HALF], U32, name="picked_pairs%d" % hf, offset=81920 - 1024, align_bytes=64)
-            nc.vector.tensor_copy(pairs[:], table[:].bitcast(U32).indirect(listed))
-            words = held.tile([P, PASSES, 2 * HALF], U8, name="picked_words%d" % hf, align_bytes=64)
-            parted = pairs[:].bitcast(U16).rearrange("p (j a) -> p a j", a=PASSES)
-            for lo, hi in ((0, P), (P, HALF)) if hf == 0 else ((0, HALF),):
-                nc.vector.tensor_copy(words[:].bitcast(U16)[:, :, lo:hi], parted[:, :, lo:hi])
+        for half, pieces in enumerate((((0, P), (P, HALF)), ((0, HALF),))):
+            pairs = shared.tile([P, HALF], U32, name="pairs%d" % half, offset=GATES_END - 2 * HALF, align_bytes=64)
+            nc.vector.tensor_copy(pairs[:], table[:].bitcast(U32).indirect(entries(half * HALF, HALF)))
+            words = held.tile([P, PASSES, 2 * HALF], U8, name="picked_words%d" % half, align_bytes=64)
+            by_pass = pairs[:].bitcast(U16).rearrange("p (j a) -> p a j", a=PASSES)
+            for lo, hi in pieces:
+                nc.vector.tensor_copy(words[:].bitcast(U16)[:, :, lo:hi], by_pass[:, :, lo:hi])
             picked_words.append(words)
 
         gate_rows = gT.rearrange("(p t) c -> t p c", t=4)
         gates = [
-            reused.tile([P, T], F32, name="gate%d" % t, offset=at, align_bytes=64)
-            for t, at in enumerate((8192, 24576, 49152, 65536))
+            shared.tile([P, T], F32, name="gate%d" % t, offset=at, align_bytes=64)
+            for t, at in enumerate((GATE0_AT, GATE1_AT, GATE2_AT, GATE3_AT))
         ]
         for t in range(4):
             nc.sync.dma_start(gates[t][:], gate_rows[t])
-        wd = reused.tile([P, 4, 2 * P], U8, name="wd", offset=81920, align_bytes=64)
+
+        wd = held.tile([P, 4, 2 * P], U8, name="wd", tag="window", align_bytes=64)
         nc.vector.tensor_copy(wd[:].bitcast(U16), wd_raw[:].bitcast(U16).rearrange("p (m t) -> p t m", t=4))
-        wd_scale = held.tile([P, 4, P], U8, name="wd_scale", align_bytes=64)
+        wd_scale = shared.tile([P, 4, P], U8, name="wd_scale", offset=GATES_END, align_bytes=64)
         nc.vector.tensor_copy(
             wd_scale[:].rearrange("p t (h m) -> p t h m", h=2),
-            planes[:, :, WD_AT:PLANE].rearrange("p h (m t) -> p t h m", t=4),
+            planes[:, :, WD_AT:PLANES].rearrange("p h (m t) -> p t h m", t=4),
         )
 
-        y_rows = [held.tile([P, 4, CHUNK], F32, name="y_rows%d" % c) for c in range(CHUNKS)]
         out_codes = held.tile([P, J], I32, name="out_codes", align_bytes=64)
         out_scales = held.tile([P, J], U8, name="out_scales", align_bytes=64)
+        out_rows = out_0.rearrange("(p t) j -> p t j", t=4)
+        word_rows = out_1[0].rearrange("p j i -> p (j i)").bitcast(I32)
+        early_gates = held.tile([P, 2, HALF], F32, name="early_gates")
+        h_tiles, quantized = [], []
 
-        def first_stage(jt):
-            hf, col = divmod(jt * P, HALF)
+        def ring_activated():
+            return ring.tile([P, 2, P, 2], F32, name="activated", bufs=4, align_bytes=64)
+
+        def ring_h():
+            return ring.tile([P, 2, P, 2], BF16, name="h", bufs=5, align_bytes=64)
+
+        def first_stage(jt, activated, h):
+            half, col = divmod(jt * P, HALF)
             sums = []
             for m in range(2):
                 acc = psum.tile([P, R], F32, name="sum%d" % m, bufs=2 + m)
                 for a in range(PASSES):
                     nc.tensor.matmul_mx(
                         out=acc[:],
-                        lhsT=picked_words[hf][:, a, 2 * col : 2 * (col + P)].bitcast(FP4X4),
+                        lhsT=picked_words[half][:, a, 2 * col : 2 * (col + P)].bitcast(FP4X4),
                         lhsT_scale=planes[:, a, jt * P : (jt + 1) * P],
                         rhs=up_weights[m][a].bitcast(FP8X4),
                         rhs_scale=planes[:, a, WG_AT + m * R : WG_AT + (m + 1) * R],
@@ -141,122 +160,129 @@ def tile_list_gmlpt_gelu_gateP_kernel(
                         stop=(a == PASSES - 1),
                     )
                 sums.append(acc[:].rearrange("p (m u e) -> p u m e", u=2, e=2))
-            if jt >= 6:
-                activated = held.tile([P, 2, P, 2], F32, name="activated%d" % jt, tag=("round0", "low1")[jt - 6], align_bytes=64)
-            else:
-                activated = ring.tile([P, 2, P, 2], F32, name="activated", bufs=4, align_bytes=64)
             nc.scalar.activation(activated[:], sums[0], GELU)
-            h = ring.tile([P, 2, P, 2], BF16, name="h", bufs=5)
             nc.vector.tensor_tensor(h[:], sums[1], activated[:], MULT)
-            return h
+            h_tiles.append(h)
 
-        def turn(pair, grouped):
-            turned = psum.tile([P, 2, 2, P], F32, name="turned", bufs=1)
-            for i, h in enumerate(pair):
-                words = h[:].rearrange("p u m e -> p (u m e)").bitcast(F32)
+        def quantize_h(c, grouped):
+            codes = held.tile([P, CHUNK], U32, name="h_codes%d" % c, align_bytes=64)
+            scales = held.tile([P, CHUNK], U8, name="h_scales%d" % c, align_bytes=64)
+            turned = psum.tile([P, 2, 2, P], F32, name="turned")
+            for i, h in enumerate(h_tiles[2 * c : 2 * c + 2]):
+                h_words = h[:].rearrange("p u m e -> p (u m e)").bitcast(F32)
                 for u in range(2):
-                    nc.tensor.transpose(turned[:, i, u, :], words[:, u * P : (u + 1) * P], identity[:])
-            nc.scalar.copy(grouped.rearrange("p (i j) u -> p i j u", i=2), turned[:].rearrange("p i u j -> p i j u"))
-
-        def second_stage(c, first):
-            codes, scales = quantized[c]
-            if True:
-                if first == 2 and c < 3:
-                    y = psum.tile([P, 2, CHUNK], F32, name="y_late", tag="sum1", bufs=3)
-                else:
-                    y = psum.tile([P, 2, CHUNK], F32, name="y", bufs=2)
-                for i in range(2):
-                    nc.tensor.matmul_mx(
-                        out=y[:, i, :],
-                        lhsT=wd[:, first + i, :].bitcast(FP4X4),
-                        lhsT_scale=wd_scale[:, first + i, :],
-                        rhs=codes[:].bitcast(FP8X4),
-                        rhs_scale=scales[:],
-                        start=True,
-                        stop=True,
-                    )
-                if first == 0 and c >= 2:
-                    kept[c] = y
-                else:
-                    nc.scalar.copy(y_rows[c][:, first : first + 2, :], y[:])
-
-        def quantize_h(c, pair):
-            if c == 3:
-                grouped = reused.tile([P, CHUNK, 2], F32, name="grouped3", offset=LAST_AT - 1024, align_bytes=64)
-            else:
-                grouped = held.tile([P, CHUNK, 2], F32, name="grouped%d" % c, align_bytes=64)
-            codes = ring.tile([P, CHUNK], U32, name="h_codes", align_bytes=64, bufs=4)
-            scales = ring.tile([P, CHUNK], U8, name="h_scales", align_bytes=64, bufs=4)
-            turn(pair, grouped[:])
+                    nc.tensor.transpose(turned[:, i, u, :], h_words[:, u * P : (u + 1) * P], identity[:])
+            nc.scalar.copy(grouped[:].rearrange("p (i j) u -> p i j u", i=2), turned[:].rearrange("p i u j -> p i j u"))
             nc.vector.quantize_mx(
                 out=codes[:].bitcast(FP8X4),
                 scales=scales[:],
                 in_=grouped[:].rearrange("p j u -> p (j u)").bitcast(BF16),
             )
-            return codes, scales
+            quantized.append((codes, scales))
 
-        h_tiles, quantized, kept = [], [], [None] * CHUNKS
-        for step in range(2 * CHUNKS + 3):
-            if step < 2 * CHUNKS:
-                h_tiles.append(first_stage(step))
-            if step >= 3 and step % 2 == 1:
-                c = (step - 3) // 2
-                quantized.append(quantize_h(c, h_tiles[2 * c : 2 * c + 2]))
-            if step >= 4 and step % 2 == 0:
-                c = (step - 4) // 2
-                second_stage(c, 0)
+        def own_grouped(c):
+            return held.tile([P, CHUNK, 2], F32, name="grouped%d" % c, align_bytes=64)
 
-        early = held.tile([P, 2, HALF], F32, name="early")
+        def y_bank():
+            return psum.tile([P, 2, CHUNK], F32, name="y", bufs=2)
+
+        def freed_bank():
+            return psum.tile([P, 2, CHUNK], F32, name="y_late", tag="sum1", bufs=3)
+
+        def second_stage(c, first, y):
+            codes, scales = quantized[c]
+            for i in range(2):
+                nc.tensor.matmul_mx(
+                    out=y[:, i, :],
+                    lhsT=wd[:, first + i, :].bitcast(FP4X4),
+                    lhsT_scale=wd_scale[:, first + i, :],
+                    rhs=codes[:].bitcast(FP8X4),
+                    rhs_scale=scales[:],
+                    start=True,
+                    stop=True,
+                )
+            return y
+
+        def to_sbuf(y, name):
+            y_rows = ring.tile([P, 2, CHUNK], F32, name=name, align_bytes=64)
+            nc.scalar.copy(y_rows[:], y[:])
+            return y_rows
+
+        def gated(t, c, product, y_row):
+            nc.vector.tensor_tensor(product, gates[t][:].indirect(entries(c * CHUNK, CHUNK)), y_row, MULT)
+
+        def round_pair(target, first, products):
+            nc.scalar.copy(target[:, :, first : first + 2], products.rearrange("p t j -> p j t"))
+
+        low0 = held.tile([P, 2, CHUNK], F32, name="low0", align_bytes=64)
+        for jt in range(4):
+            first_stage(jt, ring_activated(), ring_h())
+        quantize_h(0, own_grouped(0))
+        for jt in range(4, 6):
+            first_stage(jt, ring_activated(), ring_h())
+        y_low0 = to_sbuf(second_stage(0, 0, y_bank()), "y_low0")
+        quantize_h(1, own_grouped(1))
+        activated6 = ring.tile([P, 2, P, 2], F32, name="activated6", tag="rounded0", align_bytes=64)
+        first_stage(6, activated6, ring_h())
+
         for t in range(2):
-            nc.vector.tensor_copy(early[:, t, :], gates[t][:].indirect(entries(HALF, HALF)))
-        for c in range(CHUNKS - 1):
-            second_stage(c, 2)
+            nc.vector.tensor_copy(early_gates[:, t, :], gates[t][:].indirect(entries(HALF, HALF)))
+            gated(t, 0, low0[:, t, :], y_low0[:, t, :])
 
-        late = reused.tile([P, 2 * J + 2 * CHUNK], F32, name="late", offset=LAST_AT, align_bytes=64)
+        activated7 = ring.tile([P, 2, P, 2], F32, name="activated7", tag="low1", align_bytes=64)
+        h7 = ring.tile([P, 2, P, 2], BF16, name="h7", tag="y_low0", align_bytes=64)
+        first_stage(7, activated7, h7)
+        y_low1 = to_sbuf(second_stage(1, 0, y_bank()), "y_low1")
+        quantize_h(2, own_grouped(2))
+        low_banks = [second_stage(2, 0, y_bank())]
+        quantize_h(3, shared.tile([P, CHUNK, 2], F32, name="grouped3", offset=LATE_AT - 4 * CHUNK, align_bytes=64))
+        low_banks.append(second_stage(3, 0, y_bank()))
+        y_high = [to_sbuf(second_stage(c, 2, freed_bank()), "y_high%d" % c) for c in range(CHUNKS - 1)]
+
+        late = shared.tile([P, 2 * J + 2 * CHUNK], F32, name="late", offset=LATE_AT, align_bytes=64)
         high = late[:, 0 : 2 * J].rearrange("p (t j) -> p t j", t=2)
-        low = [
-            late[:, 2 * J :].rearrange("p (t j) -> p t j", t=2) if c == 2 else held.tile([P, 2, CHUNK], F32, name="low%d" % c, tag="low%d" % c, align_bytes=64)[:]
-            for c in range(CHUNKS)
-        ]
-        middle = reused.tile([P, 2, CHUNK, 4], BF16, name="middle", offset=LAST_AT - 4096, align_bytes=64)
-        rounded = [
-            middle[:, c - 1, :, :] if c in (1, 2) else held.tile([P, CHUNK, 4], BF16, name="rounded%d" % c, tag="round%d" % c, align_bytes=64)[:]
-            for c in range(CHUNKS)
-        ]
-        out_rows = out_0.rearrange("(p t) j -> p t j", t=4)
-        word_rows = out_1[0].rearrange("p j i -> p (j i)").bitcast(I32)
+        low1 = ring.tile([P, 2, CHUNK], F32, name="low1", align_bytes=64)
+        low3 = held.tile([P, 2, CHUNK], F32, name="low3", align_bytes=64)
+        low = [low0[:], low1[:], late[:, 2 * J :].rearrange("p (t j) -> p t j", t=2), low3[:]]
+        rounded0 = ring.tile([P, CHUNK, 4], BF16, name="rounded0", align_bytes=64)
+        middle = shared.tile([P, 2, CHUNK, 4], BF16, name="middle", offset=LATE_AT - 16 * CHUNK, align_bytes=64)
+        rounded3 = held.tile([P, CHUNK, 4], BF16, name="rounded3", align_bytes=64)
+        rounded = [rounded0[:], middle[:, 0, :, :], middle[:, 1, :, :], rounded3[:]]
 
-        def gated(t, c, product):
-            gate = gates[t][:].indirect(entries(c * CHUNK, CHUNK))
-            nc.vector.tensor_tensor(product, gate, y_rows[c][:, t, :], MULT)
+        def finish_low(c):
+            round_pair(rounded[c], 0, low[c])
+            nc.sync.dma_start(out_rows[:, 0:2, chunk(c)], low[c])
+            gated(2, c, high[:, 0, chunk(c)], y_high[c][:, 0, :])
 
-        for c in range(CHUNKS):
-            cols = slice(c * CHUNK, (c + 1) * CHUNK)
-            if c == CHUNKS - 1:
-                second_stage(c, 2)
-            if c >= 2:
-                nc.vector.tensor_tensor(low[c], kept[c][:], early[:, :, (c - 2) * CHUNK : (c - 1) * CHUNK], MULT)
-            else:
-                gated(0, c, low[c][:, 0, :])
-                gated(1, c, low[c][:, 1, :])
-            nc.scalar.copy(rounded[c][:, :, 0:2], low[c].rearrange("p t j -> p j t"))
-            nc.sync.dma_start(out_rows[:, 0:2, cols], low[c])
-            gated(2, c, high[:, 0, cols])
+        finish_low(0)
+        for t in range(2):
+            gated(t, 1, low[1][:, t, :], y_low1[:, t, :])
+        finish_low(1)
+        nc.vector.tensor_tensor(low[2], low_banks[0][:], early_gates[:, :, chunk(0)], MULT)
+        finish_low(2)
+        y_high.append(to_sbuf(second_stage(3, 2, y_bank()), "y_high3"))
+        nc.vector.tensor_tensor(low[3], low_banks[1][:], early_gates[:, :, chunk(1)], MULT)
+        finish_low(3)
         nc.sync.dma_start(out_rows[:, 2, :], high[:, 0, :])
-        for c in range(CHUNKS):
-            cols = slice(c * CHUNK, (c + 1) * CHUNK)
-            gated(3, c, high[:, 1, cols])
-            nc.scalar.copy(rounded[c][:, :, 2:4], high[:, :, cols].rearrange("p t j -> p j t"))
+
+        def finish_high(c):
+            gated(3, c, high[:, 1, chunk(c)], y_high[c][:, 1, :])
+            round_pair(rounded[c], 2, high[:, :, chunk(c)])
             nc.vector.quantize_mx(
-                out=out_codes[:, cols].bitcast(FP8X4),
-                scales=out_scales[:, cols],
+                out=out_codes[:, chunk(c)].bitcast(FP8X4),
+                scales=out_scales[:, chunk(c)],
                 in_=rounded[c].rearrange("p j t -> p (j t)"),
             )
-            if c % 2 == 1:
-                half = slice((c - 1) * CHUNK, (c + 1) * CHUNK)
-                nc.sync.dma_start(out_rows[:, 3, half], high[:, 1, half])
-            if c >= 1:
-                done = slice(0, HALF) if c == 1 else cols
-                nc.sync.dma_start(word_rows[:, done], out_codes[:, done])
-        for q in (0, 2, 1, 3):
-            nc.scalar.dma_start(out_2[0, 4 * q : 4 * q + 4, :].bitcast(I32), out_scales[32 * q : 32 * q + 4, :].bitcast(I32))
+
+        finish_high(0)
+        finish_high(1)
+        nc.sync.dma_start(out_rows[:, 3, 0:HALF], high[:, 1, 0:HALF])
+        nc.sync.dma_start(word_rows[:, 0:HALF], out_codes[:, 0:HALF])
+        finish_high(2)
+        nc.sync.dma_start(word_rows[:, chunk(2)], out_codes[:, chunk(2)])
+        finish_high(3)
+        nc.sync.dma_start(out_rows[:, 3, HALF:J], high[:, 1, HALF:J])
+        nc.sync.dma_start(word_rows[:, chunk(3)], out_codes[:, chunk(3)])
+        for q in QUADRANTS:
+            queue = nc.scalar if q < 2 else nc.sync
+            queue.dma_start(out_2[0, 4 * q : 4 * q + 4, :].bitcast(I32), out_scales[32 * q : 32 * q + 4, :].bitcast(I32))

@@ -65,14 +65,14 @@ def tile_list_gmlpt_gelu_gateP_kernel(
         nc.sync.dma_start(table_scales[rows, :].bitcast(I32), tab_scales.rearrange("a b t -> b a t").bitcast(I32))
         nc.vector.memset(table_scales[0:ROWS_AT, :].bitcast(I32), 0)
         staged = held.tile([P, PLANES], U8, name="staged", align_bytes=64)
-        nc.sync.dma_start(staged[rows, WG_AT:WU_AT].bitcast(I32), wg_scales.rearrange("a b r -> b a r").bitcast(I32))
-        nc.sync.dma_start(staged[rows, WU_AT:WD_AT].bitcast(I32), wu_scales.rearrange("a b r -> b a r").bitcast(I32))
+        nc.scalar.dma_start(staged[rows, WG_AT:WU_AT].bitcast(I32), wg_scales.rearrange("a b r -> b a r").bitcast(I32))
+        nc.scalar.dma_start(staged[rows, WU_AT:WD_AT].bitcast(I32), wu_scales.rearrange("a b r -> b a r").bitcast(I32))
         nc.sync.dma_start(staged[rows, WD_AT:PLANES].bitcast(I32), wd_scales[0].rearrange("b (h n) -> (b h) n", h=2).bitcast(I32))
 
-        wd_raw = held.tile([P, N // 2], I32, name="wd_raw", align_bytes=64)
-        nc.sync.dma_start(wd_raw[:], wd_words[0].bitcast(I32))
         table = shared.tile([P, T], I32, name="table", offset=TABLE_AT, align_bytes=64)
         nc.sync.dma_start(table[:], tab_words[0].rearrange("p t b -> p (t b)").bitcast(I32))
+        wd_raw = held.tile([P, N // 2], I32, name="wd_raw", align_bytes=64)
+        nc.sync.dma_start(wd_raw[:], wd_words[0].bitcast(I32))
         wg_first = held.tile([P, R], I32, name="wg_first", align_bytes=64)
         nc.sync.dma_start(wg_first[:], wg_words[0].rearrange("p r i -> p (r i)").bitcast(I32))
 
@@ -105,15 +105,29 @@ def tile_list_gmlpt_gelu_gateP_kernel(
                 stop=True,
             )
 
-        picked_words = []
-        for half, pieces in enumerate((((0, P), (P, HALF)), ((0, HALF),))):
+        def gather_pairs(half):
             pairs = shared.tile([P, HALF], U32, name="pairs%d" % half, offset=GATES_END - 2 * HALF, align_bytes=64)
             nc.vector.tensor_copy(pairs[:], table[:].bitcast(U32).indirect(entries(half * HALF, HALF)))
+            return pairs
+
+        def part(half, pairs, pieces):
             words = held.tile([P, PASSES, 2 * HALF], U8, name="picked_words%d" % half, align_bytes=64)
             by_pass = pairs[:].bitcast(U16).rearrange("p (j a) -> p a j", a=PASSES)
             for lo, hi in pieces:
                 nc.vector.tensor_copy(words[:].bitcast(U16)[:, :, lo:hi], by_pass[:, :, lo:hi])
-            picked_words.append(words)
+            return words
+
+        pairs = gather_pairs(0)
+        wd = held.tile([P, 4, 2 * P], U8, name="wd", tag="window", align_bytes=64)
+        nc.vector.tensor_copy(wd[:].bitcast(U16), wd_raw[:].bitcast(U16).rearrange("p (m t) -> p t m", t=4))
+        picked_words = [part(0, pairs, ((0, P), (P, HALF)))]
+        pairs = gather_pairs(1)
+        wd_scale = shared.tile([P, 4, P], U8, name="wd_scale", offset=TABLE_AT + 2 * OVERLAP, align_bytes=64)
+        nc.vector.tensor_copy(
+            wd_scale[:].rearrange("p t (h m) -> p t h m", h=2),
+            planes[:, :, WD_AT:PLANES].rearrange("p h (m t) -> p t h m", t=4),
+        )
+        picked_words.append(part(1, pairs, ((0, HALF),)))
 
         gate_rows = gT.rearrange("(p t) c -> t p c", t=4)
         gates = [
@@ -122,14 +136,6 @@ def tile_list_gmlpt_gelu_gateP_kernel(
         ]
         for t in range(4):
             nc.sync.dma_start(gates[t][:], gate_rows[t])
-
-        wd = held.tile([P, 4, 2 * P], U8, name="wd", tag="window", align_bytes=64)
-        nc.vector.tensor_copy(wd[:].bitcast(U16), wd_raw[:].bitcast(U16).rearrange("p (m t) -> p t m", t=4))
-        wd_scale = shared.tile([P, 4, P], U8, name="wd_scale", offset=GATES_END, align_bytes=64)
-        nc.vector.tensor_copy(
-            wd_scale[:].rearrange("p t (h m) -> p t h m", h=2),
-            planes[:, :, WD_AT:PLANES].rearrange("p h (m t) -> p t h m", t=4),
-        )
 
         out_codes = held.tile([P, J], I32, name="out_codes", align_bytes=64)
         out_scales = held.tile([P, J], U8, name="out_scales", align_bytes=64)

@@ -1,7 +1,6 @@
 from contextlib import ExitStack
 
 import concourse.mybir as mybir
-from concourse.masks import make_identity
 
 K, R, N, T, J = 1024, 512, 512, 4096, 1024
 FLOPS = 2 * J * (2 * K * R + R * N)
@@ -30,15 +29,15 @@ PLANES = WD_AT + N // 2
 ROWS_AT = 96
 QUADRANTS = (0, 2, 1, 3)
 
+WORD_BYTES = 4 * R
 GATE_BYTES = 4 * T
 OVERLAP = 4096
-GATE0_AT = 8192
+GATE0_AT = 4 * WORD_BYTES
 GATE1_AT = GATE0_AT + GATE_BYTES
 TABLE_AT = GATE1_AT + GATE_BYTES - OVERLAP
 GATE2_AT = TABLE_AT + GATE_BYTES - OVERLAP
 GATE3_AT = GATE2_AT + GATE_BYTES
-GATES_END = GATE3_AT + GATE_BYTES
-LATE_AT = GATES_END + 8192
+PAIRS_AT = GATE3_AT + GATE_BYTES - WORD_BYTES
 
 
 def tile_list_gmlpt_gelu_gateP_kernel(
@@ -48,7 +47,6 @@ def tile_list_gmlpt_gelu_gateP_kernel(
     with ExitStack() as ctx:
         held = ctx.enter_context(tc.tile_pool(name="held", bufs=1))
         shared = ctx.enter_context(tc.tile_pool(name="shared", bufs=1))
-        ring = ctx.enter_context(tc.tile_pool(name="ring", bufs=1))
         psum = ctx.enter_context(tc.psum_pool(name="psum", bufs=1))
 
         offsets = held.tile([P, J // 16], U16, name="offsets")
@@ -61,73 +59,108 @@ def tile_list_gmlpt_gelu_gateP_kernel(
             return slice(c * CHUNK, (c + 1) * CHUNK)
 
         rows = slice(ROWS_AT, P)
-        table_scales = held.tile([P, T], U8, name="table_scales", tag="window", align_bytes=64)
+        table_scales = held.tile([P, T], U8, name="table_scales", align_bytes=64)
         nc.sync.dma_start(table_scales[rows, :].bitcast(I32), tab_scales.rearrange("a b t -> b a t").bitcast(I32))
-        nc.vector.memset(table_scales[0:ROWS_AT, :].bitcast(I32), 0)
+        wg_rows = held.tile([P, R], U8, name="wg_rows", align_bytes=64)
         staged = held.tile([P, PLANES], U8, name="staged", align_bytes=64)
-        nc.scalar.dma_start(staged[rows, WG_AT:WU_AT].bitcast(I32), wg_scales.rearrange("a b r -> b a r").bitcast(I32))
+        nc.scalar.dma_start(wg_rows[rows, :].bitcast(I32), wg_scales.rearrange("a b r -> b a r").bitcast(I32))
         nc.scalar.dma_start(staged[rows, WU_AT:WD_AT].bitcast(I32), wu_scales.rearrange("a b r -> b a r").bitcast(I32))
         nc.sync.dma_start(staged[rows, WD_AT:PLANES].bitcast(I32), wd_scales[0].rearrange("b (h n) -> (b h) n", h=2).bitcast(I32))
+        nc.vector.memset(wg_rows[0:ROWS_AT, :].bitcast(I32), 0)
+        nc.vector.memset(table_scales[0:ROWS_AT, :].bitcast(I32), 0)
+        zero = held.tile([P, 2], F32, name="zero")
+        nc.gpsimd.memset(zero[:, 0:1], 0.0)
+        nc.scalar.activation(zero[:, 1:2], zero[:, 0:1], GELU)
+        planes = held.tile([P, PASSES, PLANES], U8, name="planes", align_bytes=64)
+        nc.vector.memset(planes[:].bitcast(I32), 0)
 
         table = shared.tile([P, T], I32, name="table", offset=TABLE_AT, align_bytes=64)
         nc.sync.dma_start(table[:], tab_words[0].rearrange("p t b -> p (t b)").bitcast(I32))
-        wd_raw = held.tile([P, N // 2], I32, name="wd_raw", align_bytes=64)
-        nc.sync.dma_start(wd_raw[:], wd_words[0].bitcast(I32))
-        wg_first = held.tile([P, R], I32, name="wg_first", align_bytes=64)
-        nc.sync.dma_start(wg_first[:], wg_words[0].rearrange("p r i -> p (r i)").bitcast(I32))
 
-        planes = held.tile([P, PASSES, PLANES], U8, name="planes", align_bytes=64)
-        nc.vector.memset(planes[:].bitcast(I32), 0)
-        identity = held.tile([P, P], F32, name="identity")
-        make_identity(nc, identity[:])
+        def load_words(name, source, at):
+            raw = shared.tile([P, R], I32, name=name, offset=at, align_bytes=64)
+            nc.sync.dma_start(raw[:], source.rearrange("p r i -> p (r i)").bitcast(I32))
+            return raw
 
-        picked_rows = shared.tile([P, J], U8, name="picked_rows", offset=GATE0_AT - J // 2, align_bytes=64)
-        nc.vector.tensor_copy(picked_rows[:], table_scales[:].indirect(offsets[:]))
-        nc.vector.tensor_copy(staged[:, 0:J].bitcast(I32), picked_rows[:].bitcast(I32))
+        wg0_raw = load_words("wg0_raw", wg_words[0], PAIRS_AT + WORD_BYTES)
+
+        nc.vector.tensor_copy(
+            staged[:, WG_AT:WU_AT].rearrange("p (t m) -> p t m", t=4),
+            wg_rows[:].rearrange("p (m t) -> p t m", t=4),
+        )
+        picked_rows = shared.tile([P, GATE0_AT + 64], U8, name="picked_rows", offset=0, align_bytes=64)
+        nc.vector.tensor_copy(picked_rows[:, 0:J], table_scales[:].indirect(offsets[:]))
+        nc.vector.tensor_copy(staged[:, 0:J].bitcast(I32), picked_rows[:, 0:J].bitcast(I32))
         for q in QUADRANTS:
             first = ROWS_AT + 8 * q
             nc.sync.dma_start(planes[32 * q : 32 * q + 4, :, :].bitcast(I32), staged[first : first + 8, :].bitcast(I32))
 
-        later = shared.tile([P, 1 + PASSES, R], I32, name="later", offset=GATE0_AT - (1 + PASSES) * 4 * R, align_bytes=64)
-        nc.sync.dma_start(later[:, 0, :], wg_words[1].rearrange("p r i -> p (r i)").bitcast(I32))
-        nc.sync.dma_start(later[:, 1:, :], wu_words.rearrange("a p r i -> p a (r i)").bitcast(I32))
-        up_weights = ((wg_first[:], later[:, 0, :]), (later[:, 1, :], later[:, 2, :]))
-
-        unread = psum.tile([P, R], F32, name="unread", tag="y", bufs=2)
+        unread = psum.tile([P, R], F32, name="unread", tag="y", bufs=3)
         for repeat in range(2):
             nc.tensor.matmul_mx(
                 out=unread[:],
-                lhsT=wd_raw[:, 0 : P // 2].bitcast(FP4X4),
+                lhsT=wg0_raw[:, 0 : P // 2].bitcast(FP4X4),
                 lhsT_scale=staged[:, 0:P],
-                rhs=wg_first[:].bitcast(FP8X4),
+                rhs=wg0_raw[:].bitcast(FP8X4),
                 rhs_scale=staged[:, 0:R],
                 start=True,
                 stop=True,
             )
 
-        def gather_pairs(half):
-            pairs = shared.tile([P, HALF], U32, name="pairs%d" % half, offset=GATES_END - 2 * HALF, align_bytes=64)
-            nc.vector.tensor_copy(pairs[:], table[:].bitcast(U32).indirect(entries(half * HALF, HALF)))
-            return pairs
+        wg1_raw = load_words("wg1_raw", wg_words[1], 0)
+        wu_raw = shared.tile([P, PASSES * R], I32, name="wu_raw", offset=WORD_BYTES, align_bytes=64)
+        for a in range(PASSES):
+            nc.sync.dma_start(wu_raw[:, a * R : (a + 1) * R], wu_words[a].rearrange("p r i -> p (r i)").bitcast(I32))
+        wu0_raw, wu1_raw = wu_raw[:, 0:R], wu_raw[:, R : 2 * R]
+        wd_raw = shared.tile([P, N // 2], I32, name="wd_raw", offset=3 * WORD_BYTES, align_bytes=64)
+        nc.sync.dma_start(wd_raw[:], wd_words[0].bitcast(I32))
 
-        def part(half, pairs, pieces):
-            words = held.tile([P, PASSES, 2 * HALF], U8, name="picked_words%d" % half, align_bytes=64)
-            by_pass = pairs[:].bitcast(U16).rearrange("p (j a) -> p a j", a=PASSES)
-            for lo, hi in pieces:
-                nc.vector.tensor_copy(words[:].bitcast(U16)[:, :, lo:hi], by_pass[:, :, lo:hi])
-            return words
+        def gather_pairs(pairs, start, count):
+            nc.vector.tensor_copy(pairs[:], table[:].bitcast(U32).indirect(entries(start, count)))
 
-        pairs = gather_pairs(0)
-        wd = held.tile([P, 4, 2 * P], U8, name="wd", tag="window", align_bytes=64)
-        nc.vector.tensor_copy(wd[:].bitcast(U16), wd_raw[:].bitcast(U16).rearrange("p (m t) -> p t m", t=4))
-        picked_words = [part(0, pairs, ((0, P), (P, HALF)))]
-        pairs = gather_pairs(1)
-        wd_scale = shared.tile([P, 4, P], U8, name="wd_scale", offset=TABLE_AT + 2 * OVERLAP, align_bytes=64)
+        def part(words, pairs):
+            nc.vector.tensor_copy(
+                words[:].bitcast(U16).rearrange("p a (o i) -> p o a i", i=8),
+                pairs[:].bitcast(U16).rearrange("p (o i a) -> p o a i", a=PASSES, i=8),
+            )
+
+        def deal(name, raw, copy):
+            dealt = held.tile([P, R], U32, name=name, align_bytes=64)
+            copy(
+                dealt[:].rearrange("p (t o i) -> p o t i", t=4, i=4),
+                raw[:, :].bitcast(U32).rearrange("p (o i t) -> p o t i", t=4, i=4),
+            )
+            return dealt
+
+        pairs = [
+            shared.tile([P, CHUNK], U32, name="pairs0", offset=PAIRS_AT, align_bytes=64),
+            held.tile([P, CHUNK], U32, name="pairs1", align_bytes=64),
+        ]
+        words = [held.tile([P, PASSES, 2 * CHUNK], U8, name="words%d" % c, align_bytes=64) for c in range(2)]
+        gather_pairs(pairs[0], 0, CHUNK)
+        gather_pairs(pairs[1], CHUNK, CHUNK)
+        part(words[0], pairs[0])
+        wg0 = deal("wg0", wg0_raw, nc.scalar.copy)
+        part(words[1], pairs[1])
+        late_pairs = shared.tile([P, HALF], U32, name="late_pairs", offset=PAIRS_AT, align_bytes=64)
+        gather_pairs(late_pairs, HALF, HALF)
+        wg1 = deal("wg1", wg1_raw, nc.scalar.copy)
+        wu0 = deal("wu0", wu0_raw, nc.scalar.copy)
+        wu1 = deal("wu1", wu1_raw, nc.scalar.copy)
+        wu_scale = held.tile([P, PASSES, R], U8, name="wu_scale", align_bytes=64)
+        nc.vector.tensor_copy(
+            wu_scale[:].rearrange("p a (t m) -> p a t m", t=4),
+            planes[:, :, WU_AT:WD_AT].rearrange("p a (m t) -> p a t m", t=4),
+        )
+        late_words = shared.tile([P, PASSES, 2 * HALF], U8, name="late_words", offset=0, align_bytes=64)
+        part(late_words, late_pairs)
+        wd_scale = held.tile([P, 4, P], U8, name="wd_scale", align_bytes=64)
         nc.vector.tensor_copy(
             wd_scale[:].rearrange("p t (h m) -> p t h m", h=2),
             planes[:, :, WD_AT:PLANES].rearrange("p h (m t) -> p t h m", t=4),
         )
-        picked_words.append(part(1, pairs, ((0, HALF),)))
+        weight_scales = (planes[:, :, WG_AT:WU_AT], wu_scale[:])
+        weights = ((wg0, wg1), (wu0, wu1))
 
         gate_rows = gT.rearrange("(p t) c -> t p c", t=4)
         gates = [
@@ -137,71 +170,63 @@ def tile_list_gmlpt_gelu_gateP_kernel(
         for t in range(4):
             nc.sync.dma_start(gates[t][:], gate_rows[t])
 
-        out_codes = held.tile([P, J], I32, name="out_codes", align_bytes=64)
-        out_scales = held.tile([P, J], U8, name="out_scales", align_bytes=64)
-        out_rows = out_0.rearrange("(p t) j -> p t j", t=4)
-        word_rows = out_1[0].rearrange("p j i -> p (j i)").bitcast(I32)
-        early_gates = held.tile([P, 2, HALF], F32, name="early_gates")
-        h_tiles, quantized = [], []
+        def picked(jt, a):
+            if jt < 4:
+                return words[jt // 2][:, a, 2 * P * (jt % 2) : 2 * P * (jt % 2 + 1)]
+            return late_words[:, a, 2 * P * (jt - 4) : 2 * P * (jt - 3)]
 
-        def ring_activated():
-            return ring.tile([P, 2, P, 2], F32, name="activated", bufs=4, align_bytes=64)
+        def passes(bank, w, jt, a):
+            for t in range(4):
+                nc.tensor.matmul_mx(
+                    out=bank[:, t, :],
+                    lhsT=weights[w][a][:, t * P : (t + 1) * P].bitcast(FP8X4),
+                    lhsT_scale=weight_scales[w][:, a, t * P : (t + 1) * P],
+                    rhs=picked(jt, a).bitcast(FP4X4),
+                    rhs_scale=planes[:, a, jt * P : (jt + 1) * P],
+                    start=(a == 0 and t == 0),
+                    stop=(a == PASSES - 1 and t == 3),
+                )
 
-        def ring_h():
-            return ring.tile([P, 2, P, 2], BF16, name="h", bufs=5, align_bytes=64)
+        def new_bank(w):
+            return psum.tile([P, 4, P], F32, name="sum%d" % w, bufs=2 + w)
 
-        def first_stage(jt, activated, h):
-            half, col = divmod(jt * P, HALF)
-            sums = []
-            for m in range(2):
-                acc = psum.tile([P, R], F32, name="sum%d" % m, bufs=2 + m)
-                for a in range(PASSES):
-                    nc.tensor.matmul_mx(
-                        out=acc[:],
-                        lhsT=picked_words[half][:, a, 2 * col : 2 * (col + P)].bitcast(FP4X4),
-                        lhsT_scale=planes[:, a, jt * P : (jt + 1) * P],
-                        rhs=up_weights[m][a].bitcast(FP8X4),
-                        rhs_scale=planes[:, a, WG_AT + m * R : WG_AT + (m + 1) * R],
-                        start=(a == 0),
-                        stop=(a == PASSES - 1),
-                    )
-                sums.append(acc[:].rearrange("p (m u e) -> p u m e", u=2, e=2))
-            nc.scalar.activation(activated[:], sums[0], GELU)
-            nc.vector.tensor_tensor(h[:], sums[1], activated[:], MULT)
-            h_tiles.append(h)
+        def by_entry(flat):
+            return flat.rearrange("p (j t) -> p j t", t=4)
 
-        def quantize_h(c, grouped):
+        def gelu(bank, activated):
+            nc.scalar.activation(by_entry(activated), bank[:].rearrange("p t j -> p j t"), GELU)
+
+        def gate_sum(jt, activated):
+            bank = new_bank(0)
+            for a in range(PASSES):
+                passes(bank, 0, jt, a)
+            gelu(bank, activated)
+
+        def up_sum(jt):
+            bank = new_bank(1)
+            for a in range(PASSES):
+                passes(bank, 1, jt, a)
+            return bank
+
+        def h_product(bank, activated, h):
+            nc.vector.tensor_tensor(by_entry(h), bank[:].rearrange("p t j -> p j t"), by_entry(activated), MULT)
+
+        quantized = []
+
+        def quantize_h(c, h):
             codes = held.tile([P, CHUNK], U32, name="h_codes%d" % c, align_bytes=64)
             scales = held.tile([P, CHUNK], U8, name="h_scales%d" % c, align_bytes=64)
-            turned = psum.tile([P, 2, 2, P], F32, name="turned")
-            for i, h in enumerate(h_tiles[2 * c : 2 * c + 2]):
-                h_words = h[:].rearrange("p u m e -> p (u m e)").bitcast(F32)
-                for u in range(2):
-                    nc.tensor.transpose(turned[:, i, u, :], h_words[:, u * P : (u + 1) * P], identity[:])
-            nc.scalar.copy(grouped[:].rearrange("p (i j) u -> p i j u", i=2), turned[:].rearrange("p i u j -> p i j u"))
-            nc.vector.quantize_mx(
-                out=codes[:].bitcast(FP8X4),
-                scales=scales[:],
-                in_=grouped[:].rearrange("p j u -> p (j u)").bitcast(BF16),
-            )
+            nc.vector.quantize_mx(out=codes[:].bitcast(FP8X4), scales=scales[:], in_=h)
             quantized.append((codes, scales))
 
-        def own_grouped(c):
-            return held.tile([P, CHUNK, 2], F32, name="grouped%d" % c, align_bytes=64)
-
-        def y_bank():
-            return psum.tile([P, 2, CHUNK], F32, name="y", bufs=2)
-
-        def freed_bank():
-            return psum.tile([P, 2, CHUNK], F32, name="y_late", tag="sum1", bufs=3)
-
-        def second_stage(c, first, y):
+        def y_sums(c, slices):
             codes, scales = quantized[c]
-            for i in range(2):
+            y = psum.tile([P, 2, CHUNK], F32, name="y", bufs=3)
+            for i, t in enumerate(slices):
                 nc.tensor.matmul_mx(
                     out=y[:, i, :],
-                    lhsT=wd[:, first + i, :].bitcast(FP4X4),
-                    lhsT_scale=wd_scale[:, first + i, :],
+                    lhsT=wd[:, t, :].bitcast(FP4X4),
+                    lhsT_scale=wd_scale[:, t, :],
                     rhs=codes[:].bitcast(FP8X4),
                     rhs_scale=scales[:],
                     start=True,
@@ -209,86 +234,163 @@ def tile_list_gmlpt_gelu_gateP_kernel(
                 )
             return y
 
-        def to_sbuf(y, name):
-            y_rows = ring.tile([P, 2, CHUNK], F32, name=name, align_bytes=64)
-            nc.scalar.copy(y_rows[:], y[:])
-            return y_rows
+        def second_stage(c, slices, y_rows):
+            y = y_sums(c, slices)
+            nc.scalar.copy(y_rows, y[:].rearrange("p i j -> p (i j)"))
+            for i, t in enumerate(slices):
+                y_of[t, c] = y_rows[:, i * CHUNK : (i + 1) * CHUNK]
 
-        def gated(t, c, product, y_row):
-            nc.vector.tensor_tensor(product, gates[t][:].indirect(entries(c * CHUNK, CHUNK)), y_row, MULT)
+        y_of = {}
+        work = held.tile([P, 17 * P], F32, name="work", align_bytes=64)
 
-        def round_pair(target, first, products):
-            nc.scalar.copy(target[:, :, first : first + 2], products.rearrange("p t j -> p j t"))
+        def cells(first, count):
+            return work[:, first * P : (first + count) * P]
 
-        low0 = held.tile([P, 2, CHUNK], F32, name="low0", align_bytes=64)
-        for jt in range(4):
-            first_stage(jt, ring_activated(), ring_h())
-        quantize_h(0, own_grouped(0))
-        for jt in range(4, 6):
-            first_stage(jt, ring_activated(), ring_h())
-        y_low0 = to_sbuf(second_stage(0, 0, y_bank()), "y_low0")
-        quantize_h(1, own_grouped(1))
-        activated6 = ring.tile([P, 2, P, 2], F32, name="activated6", tag="rounded0", align_bytes=64)
-        first_stage(6, activated6, ring_h())
+        low = held.tile([P, 2 * J], F32, name="low", align_bytes=64)
+        high = held.tile([P, 2 * J], F32, name="high", align_bytes=64)
 
-        for t in range(2):
-            nc.vector.tensor_copy(early_gates[:, t, :], gates[t][:].indirect(entries(HALF, HALF)))
-            gated(t, 0, low0[:, t, :], y_low0[:, t, :])
+        def span(tile, first, count):
+            return tile[:, first * CHUNK : (first + count) * CHUNK]
 
-        activated7 = ring.tile([P, 2, P, 2], F32, name="activated7", tag="low1", align_bytes=64)
-        h7 = ring.tile([P, 2, P, 2], BF16, name="h7", tag="y_low0", align_bytes=64)
-        first_stage(7, activated7, h7)
-        y_low1 = to_sbuf(second_stage(1, 0, y_bank()), "y_low1")
-        quantize_h(2, own_grouped(2))
-        low_banks = [second_stage(2, 0, y_bank())]
-        quantize_h(3, shared.tile([P, CHUNK, 2], F32, name="grouped3", offset=LATE_AT - 4 * CHUNK, align_bytes=64))
-        low_banks.append(second_stage(3, 0, y_bank()))
-        y_high = [to_sbuf(second_stage(c, 2, freed_bank()), "y_high%d" % c) for c in range(CHUNKS - 1)]
+        def product(t, c):
+            if t < 2:
+                return span(low, 4 * (c // 2) + 2 * t + c % 2, 1)
+            return span(high, 4 * (t - 2) + c, 1)
 
-        late = shared.tile([P, 2 * J + 2 * CHUNK], F32, name="late", offset=LATE_AT, align_bytes=64)
-        high = late[:, 0 : 2 * J].rearrange("p (t j) -> p t j", t=2)
-        low1 = ring.tile([P, 2, CHUNK], F32, name="low1", align_bytes=64)
-        low3 = held.tile([P, 2, CHUNK], F32, name="low3", align_bytes=64)
-        low = [low0[:], low1[:], late[:, 2 * J :].rearrange("p (t j) -> p t j", t=2), low3[:]]
-        rounded0 = ring.tile([P, CHUNK, 4], BF16, name="rounded0", align_bytes=64)
-        middle = shared.tile([P, 2, CHUNK, 4], BF16, name="middle", offset=LATE_AT - 16 * CHUNK, align_bytes=64)
-        rounded3 = held.tile([P, CHUNK, 4], BF16, name="rounded3", align_bytes=64)
-        rounded = [rounded0[:], middle[:, 0, :, :], middle[:, 1, :, :], rounded3[:]]
+        def look_up(t, c):
+            nc.vector.tensor_tensor(product(t, c), gates[t][:].indirect(entries(c * CHUNK, CHUNK)), y_of[t, c], MULT)
 
-        def finish_low(c):
-            round_pair(rounded[c], 0, low[c])
-            nc.sync.dma_start(out_rows[:, 0:2, chunk(c)], low[c])
-            gated(2, c, high[:, 0, chunk(c)], y_high[c][:, 0, :])
+        def own(name, count):
+            tile = held.tile([P, count * CHUNK], F32, name=name, align_bytes=64)
+            return tile[:]
 
-        finish_low(0)
-        for t in range(2):
-            gated(t, 1, low[1][:, t, :], y_low1[:, t, :])
-        finish_low(1)
-        nc.vector.tensor_tensor(low[2], low_banks[0][:], early_gates[:, :, chunk(0)], MULT)
-        finish_low(2)
-        y_high.append(to_sbuf(second_stage(3, 2, y_bank()), "y_high3"))
-        nc.vector.tensor_tensor(low[3], low_banks[1][:], early_gates[:, :, chunk(1)], MULT)
-        finish_low(3)
-        nc.sync.dma_start(out_rows[:, 2, :], high[:, 0, :])
+        rounded = held.tile([P, 4 * J], BF16, name="rounded", align_bytes=64)
+        by_pair = rounded[:].rearrange("p (j t) -> p j t", t=4)
 
-        def finish_high(c):
-            gated(3, c, high[:, 1, chunk(c)], y_high[c][:, 1, :])
-            round_pair(rounded[c], 2, high[:, :, chunk(c)])
-            nc.vector.quantize_mx(
-                out=out_codes[:, chunk(c)].bitcast(FP8X4),
-                scales=out_scales[:, chunk(c)],
-                in_=rounded[c].rearrange("p j t -> p (j t)"),
+        def round_low(c):
+            half = span(low, 4 * (c // 2), 4).rearrange("p (t j) -> p j t", t=2)
+            nc.scalar.copy(by_pair[:, chunk(c), 0:2], half[:, chunk(c % 2), :])
+
+        first = shared.tile([P, 2 * CHUNK], F32, name="first", offset=2 * WORD_BYTES, align_bytes=64)
+        second = shared.tile([P, 2 * CHUNK], F32, name="second", offset=WORD_BYTES, align_bytes=64)
+        activated = [first[:], second[:]]
+        activated.extend((own("activated2", 2), cells(6, 4), own("activated4", 2), own("activated5", 2)))
+        activated.extend((span(low, 4, 2), span(low, 6, 2)))
+        h_chunks = [own("h0", 2), cells(0, 4), cells(4, 4), cells(10, 4)]
+        h_chunks = [h.bitcast(BF16) for h in h_chunks]
+
+        def h_of(jt):
+            return h_chunks[jt // 2][:, (jt % 2) * 4 * P : (jt % 2 + 1) * 4 * P]
+
+        def up(jt):
+            h_product(up_sum(jt), activated[jt], h_of(jt))
+
+        def tile_sums(jt):
+            gate_sum(jt, activated[jt])
+            up(jt)
+
+        def gather_ahead(c, target):
+            nc.vector.tensor_copy(target, gates[0][:].indirect(entries(c * CHUNK, CHUNK)))
+
+        def low_late(c, y_row):
+            y = y_sums(c, (0, 1))
+            nc.scalar.copy(y_row, y[:, 1, :])
+            y_of[1, c] = y_row
+            return y
+
+        out_rows = out_0.rearrange("(p t) j -> p t j", t=4)
+        word_rows = out_1[0].rearrange("p j i -> p (j i)").bitcast(I32)
+
+        banks = [new_bank(0) for jt in range(2)]
+        passes(banks[0], 0, 0, 0)
+        passes(banks[1], 0, 1, 0)
+        passes(banks[0], 0, 0, 1)
+        gelu(banks[0], activated[0])
+        up(0)
+        wd = shared.tile([P, 4, 2 * P], U8, name="wd", offset=2 * WORD_BYTES, align_bytes=64)
+        nc.scalar.copy(wd[:].bitcast(U16), wd_raw[:].bitcast(U16).rearrange("p (m t) -> p t m", t=4))
+        passes(banks[1], 0, 1, 1)
+        gelu(banks[1], activated[1])
+        up(1)
+        quantize_h(0, h_chunks[0])
+        tile_sums(2)
+        y0 = y_sums(0, (0, 1))
+        nc.scalar.copy(cells(3, 14).rearrange("p (i x) -> p i x", i=2)[:, :, 0:CHUNK], y0[:])
+        y_of[0, 0], y_of[1, 0] = cells(3, 2), cells(10, 2)
+        second_stage(0, (2, 3), own("y_high0", 2))
+        ahead3 = own("ahead3", 1)
+        gather_ahead(3, ahead3)
+        look_up(0, 0)
+        ahead2 = own("ahead2", 1)
+        gather_ahead(2, ahead2)
+        tile_sums(3)
+        tile_sums(4)
+        quantize_h(1, h_chunks[1])
+        second_stage(1, (1, 0), cells(12, 4))
+        cross = own("cross", 3)
+        second_stage(1, (3, 2), span(cross, 0, 2))
+        tile_sums(5)
+        look_up(0, 1)
+        quantize_h(2, h_chunks[2])
+        look_up(1, 0)
+        look_up(1, 1)
+        round_low(0)
+        round_low(1)
+        nc.sync.dma_start(out_rows[:, 0:2, 0:HALF], span(low, 0, 4).rearrange("p (t j) -> p t j", t=2))
+        tile_sums(6)
+        y2 = low_late(2, own("y_one2", 1))
+        second_stage(2, (2, 3), own("y_high2", 2))
+        tile_sums(7)
+        nc.vector.tensor_tensor(product(0, 2), y2[:, 0, :], ahead2, MULT)
+        quantize_h(3, h_chunks[3])
+        look_up(1, 2)
+        round_low(2)
+        look_up(2, 0)
+        y3 = low_late(3, y_of[2, 0])
+        look_up(2, 1)
+        second_stage(3, (2, 3), span(cross, 1, 2))
+        nc.vector.tensor_tensor(product(0, 3), y3[:, 0, :], ahead3, MULT)
+        look_up(1, 3)
+        round_low(3)
+        nc.sync.dma_start(out_rows[:, 0:2, HALF:J], span(low, 4, 4).rearrange("p (t j) -> p t j", t=2))
+        for c in range(2, CHUNKS):
+            look_up(2, c)
+        nc.sync.dma_start(out_rows[:, 2, :], high[:, 0:J])
+
+        out_codes = held.tile([P, J], I32, name="out_codes", align_bytes=64)
+        out_scales = held.tile([P, J], U8, name="out_scales", align_bytes=64)
+
+        high_by_entry = high[:].rearrange("p (t j) -> p j t", t=2)
+        y_three = [y_of[3, c] for c in range(CHUNKS)]
+
+        def last_look_up(lo, hi):
+            c, col = divmod(lo, CHUNK)
+            nc.vector.tensor_tensor(
+                high[:, J + lo : J + hi], gates[3][:].indirect(entries(lo, hi - lo)), y_three[c][:, col : col + hi - lo], MULT
             )
 
-        finish_high(0)
-        finish_high(1)
-        nc.sync.dma_start(out_rows[:, 3, 0:HALF], high[:, 1, 0:HALF])
-        nc.sync.dma_start(word_rows[:, 0:HALF], out_codes[:, 0:HALF])
-        finish_high(2)
-        nc.sync.dma_start(word_rows[:, chunk(2)], out_codes[:, chunk(2)])
-        finish_high(3)
-        nc.sync.dma_start(out_rows[:, 3, HALF:J], high[:, 1, HALF:J])
-        nc.sync.dma_start(word_rows[:, chunk(3)], out_codes[:, chunk(3)])
+        def round_high(lo, hi, copy):
+            copy(by_pair[:, lo:hi, 2:4], high_by_entry[:, lo:hi, :])
+
+        def quantize_out(lo, hi):
+            nc.vector.quantize_mx(
+                out=out_codes[:, lo:hi].bitcast(FP8X4), scales=out_scales[:, lo:hi], in_=rounded[:, 4 * lo : 4 * hi]
+            )
+            nc.sync.dma_start(word_rows[:, lo:hi], out_codes[:, lo:hi])
+
+        for lo, hi in ((0, P), (P, CHUNK), (CHUNK, HALF)):
+            last_look_up(lo, hi)
+            round_high(lo, hi, nc.scalar.copy)
+        nc.sync.dma_start(out_rows[:, 3, 0:HALF], high[:, J : J + HALF])
+        last_look_up(HALF, HALF + CHUNK)
+        round_high(HALF, HALF + CHUNK, nc.scalar.copy)
+        last_look_up(HALF + CHUNK, J)
+        round_high(HALF + CHUNK, J - P, nc.scalar.copy)
+        nc.sync.dma_start(out_rows[:, 3, HALF:J], high[:, J + HALF : 2 * J])
+        quantize_out(0, HALF)
+        round_high(J - P, J, nc.vector.tensor_copy)
+        quantize_out(HALF, HALF + CHUNK)
+        quantize_out(HALF + CHUNK, J)
         for q in QUADRANTS:
             queue = nc.scalar if q < 2 else nc.sync
             queue.dma_start(out_2[0, 4 * q : 4 * q + 4, :].bitcast(I32), out_scales[32 * q : 32 * q + 4, :].bitcast(I32))

@@ -127,8 +127,8 @@ def tile_list_gmlpt_gelu_gateP_kernel(
         def deal(name, raw, copy):
             dealt = held.tile([P, R], U32, name=name, align_bytes=64)
             copy(
-                dealt[:].rearrange("p (t o i) -> p o t i", t=4, i=4),
-                raw[:, :].bitcast(U32).rearrange("p (o i t) -> p o t i", t=4, i=4),
+                dealt[:].rearrange("p (t m) -> p m t", t=4),
+                raw[:, :].bitcast(U32).rearrange("p (m t) -> p m t", t=4),
             )
             return dealt
 
@@ -190,11 +190,14 @@ def tile_list_gmlpt_gelu_gateP_kernel(
         def new_bank(w):
             return psum.tile([P, 4, P], F32, name="sum%d" % w, bufs=2 + w)
 
-        def by_entry(flat):
-            return flat.rearrange("p (j t) -> p j t", t=4)
+        def in_pairs(bank):
+            return bank[:].rearrange("p t (o i) -> p o t i", i=2)
+
+        def as_read(flat):
+            return flat.rearrange("p (o t i) -> p o t i", t=4, i=2)
 
         def gelu(bank, activated):
-            nc.scalar.activation(by_entry(activated), bank[:].rearrange("p t j -> p j t"), GELU)
+            nc.scalar.activation(as_read(activated), in_pairs(bank), GELU)
 
         def gate_sum(jt, activated):
             bank = new_bank(0)
@@ -209,7 +212,7 @@ def tile_list_gmlpt_gelu_gateP_kernel(
             return bank
 
         def h_product(bank, activated, h):
-            nc.vector.tensor_tensor(by_entry(h), bank[:].rearrange("p t j -> p j t"), by_entry(activated), MULT)
+            nc.vector.tensor_tensor(h.rearrange("p (o i t) -> p o t i", t=4, i=2), in_pairs(bank), as_read(activated), MULT)
 
         quantized = []
 

@@ -32,7 +32,10 @@ QUADRANTS = (0, 2, 1, 3)
 WORD_BYTES = 4 * R
 GATE_BYTES = 4 * T
 OVERLAP = 4096
-GATE0_AT = 4 * WORD_BYTES
+SECOND_AT = 3 * WORD_BYTES // 2
+WU1_AT = SECOND_AT + WORD_BYTES
+LATE_AT = WU1_AT + 4 * P
+GATE0_AT = 5 * WORD_BYTES
 GATE1_AT = GATE0_AT + GATE_BYTES
 TABLE_AT = GATE1_AT + GATE_BYTES - OVERLAP
 GATE2_AT = TABLE_AT + GATE_BYTES - OVERLAP
@@ -108,11 +111,9 @@ def tile_list_gmlpt_gelu_gateP_kernel(
             )
 
         wg1_raw = load_words("wg1_raw", wg_words[1], 0)
-        wu_raw = shared.tile([P, PASSES * R], I32, name="wu_raw", offset=WORD_BYTES, align_bytes=64)
-        for a in range(PASSES):
-            nc.sync.dma_start(wu_raw[:, a * R : (a + 1) * R], wu_words[a].rearrange("p r i -> p (r i)").bitcast(I32))
-        wu0_raw, wu1_raw = wu_raw[:, 0:R], wu_raw[:, R : 2 * R]
-        wd_raw = shared.tile([P, N // 2], I32, name="wd_raw", offset=3 * WORD_BYTES, align_bytes=64)
+        wu0_raw = load_words("wu0_raw", wu_words[0], WORD_BYTES)
+        wu1_raw = load_words("wu1_raw", wu_words[1], WU1_AT)
+        wd_raw = shared.tile([P, N // 2], I32, name="wd_raw", offset=4 * WORD_BYTES, align_bytes=64)
         nc.sync.dma_start(wd_raw[:], wd_words[0].bitcast(I32))
 
         def gather_pairs(pairs, start, count):
@@ -146,15 +147,15 @@ def tile_list_gmlpt_gelu_gateP_kernel(
         gather_pairs(late_pairs, HALF, HALF)
         wg1 = deal("wg1", wg1_raw, nc.scalar.copy)
         wu0 = deal("wu0", wu0_raw, nc.scalar.copy)
-        wu1 = deal("wu1", wu1_raw, nc.scalar.copy)
         wu_scale = held.tile([P, PASSES, R], U8, name="wu_scale", align_bytes=64)
         nc.vector.tensor_copy(
             wu_scale[:].rearrange("p a (t m) -> p a t m", t=4),
             planes[:, :, WU_AT:WD_AT].rearrange("p a (m t) -> p a t m", t=4),
         )
-        late_words = shared.tile([P, PASSES, 2 * HALF], U8, name="late_words", offset=0, align_bytes=64)
+        wu1 = deal("wu1", wu1_raw, nc.vector.tensor_copy)
+        late_words = shared.tile([P, PASSES, 2 * HALF], U8, name="late_words", offset=LATE_AT, align_bytes=64)
         part(late_words, late_pairs)
-        wd_scale = held.tile([P, 4, P], U8, name="wd_scale", align_bytes=64)
+        wd_scale = shared.tile([P, 4, P], U8, name="wd_scale", offset=WU1_AT, align_bytes=64)
         nc.vector.tensor_copy(
             wd_scale[:].rearrange("p t (h m) -> p t h m", h=2),
             planes[:, :, WD_AT:PLANES].rearrange("p h (m t) -> p t h m", t=4),
@@ -257,7 +258,7 @@ def tile_list_gmlpt_gelu_gateP_kernel(
 
         def product(t, c):
             if t < 2:
-                return span(low, 4 * (c // 2) + 2 * t + c % 2, 1)
+                return span(low, 4 * t + c, 1)
             return span(high, 4 * (t - 2) + c, 1)
 
         def look_up(t, c):
@@ -271,14 +272,13 @@ def tile_list_gmlpt_gelu_gateP_kernel(
         by_pair = rounded[:].rearrange("p (j t) -> p j t", t=4)
 
         def round_low(c):
-            half = span(low, 4 * (c // 2), 4).rearrange("p (t j) -> p j t", t=2)
-            nc.scalar.copy(by_pair[:, chunk(c), 0:2], half[:, chunk(c % 2), :])
+            nc.scalar.copy(by_pair[:, chunk(c), 0:2], low[:].rearrange("p (t j) -> p j t", t=2)[:, chunk(c), :])
 
-        first = shared.tile([P, 2 * CHUNK], F32, name="first", offset=2 * WORD_BYTES, align_bytes=64)
-        second = shared.tile([P, 2 * CHUNK], F32, name="second", offset=WORD_BYTES, align_bytes=64)
+        first = shared.tile([P, 2 * CHUNK], F32, name="first", offset=WORD_BYTES // 2, align_bytes=64)
+        second = shared.tile([P, 2 * CHUNK], F32, name="second", offset=SECOND_AT, align_bytes=64)
         activated = [first[:], second[:]]
         activated.extend((own("activated2", 2), cells(6, 4), own("activated4", 2), own("activated5", 2)))
-        activated.extend((span(low, 4, 2), span(low, 6, 2)))
+        activated.extend((span(low, 2, 2), span(low, 6, 2)))
         h_chunks = [own("h0", 2), cells(0, 4), cells(4, 4), cells(10, 4)]
         h_chunks = [h.bitcast(BF16) for h in h_chunks]
 
@@ -310,7 +310,7 @@ def tile_list_gmlpt_gelu_gateP_kernel(
         passes(banks[0], 0, 0, 1)
         gelu(banks[0], activated[0])
         up(0)
-        wd = shared.tile([P, 4, 2 * P], U8, name="wd", offset=2 * WORD_BYTES, align_bytes=64)
+        wd = shared.tile([P, 4, 2 * P], U8, name="wd", offset=WORD_BYTES // 2, align_bytes=64)
         nc.scalar.copy(wd[:].bitcast(U16), wd_raw[:].bitcast(U16).rearrange("p (m t) -> p t m", t=4))
         passes(banks[1], 0, 1, 1)
         gelu(banks[1], activated[1])
@@ -335,12 +335,12 @@ def tile_list_gmlpt_gelu_gateP_kernel(
         tile_sums(5)
         look_up(0, 1)
         quantize_h(2, h_chunks[2])
+        gate_sum(6, activated[6])
         look_up(1, 0)
         look_up(1, 1)
         round_low(0)
         round_low(1)
-        nc.sync.dma_start(out_rows[:, 0:2, 0:HALF], span(low, 0, 4).rearrange("p (t j) -> p t j", t=2))
-        tile_sums(6)
+        up(6)
         y2 = low_late(2, own("y_one2", 1))
         second_stage(2, (2, 3), own("y_high2", 2))
         tile_sums(7)
@@ -353,9 +353,10 @@ def tile_list_gmlpt_gelu_gateP_kernel(
         look_up(2, 1)
         second_stage(3, (2, 3), span(cross, 1, 2))
         nc.vector.tensor_tensor(product(0, 3), y3[:, 0, :], ahead3, MULT)
+        nc.sync.dma_start(out_rows[:, 0, :], low[:, 0:J])
         look_up(1, 3)
         round_low(3)
-        nc.sync.dma_start(out_rows[:, 0:2, HALF:J], span(low, 4, 4).rearrange("p (t j) -> p t j", t=2))
+        nc.sync.dma_start(out_rows[:, 1, :], low[:, J : 2 * J])
         for c in range(2, CHUNKS):
             look_up(2, c)
         nc.sync.dma_start(out_rows[:, 2, :], high[:, 0:J])
@@ -379,21 +380,20 @@ def tile_list_gmlpt_gelu_gateP_kernel(
             nc.vector.quantize_mx(
                 out=out_codes[:, lo:hi].bitcast(FP8X4), scales=out_scales[:, lo:hi], in_=rounded[:, 4 * lo : 4 * hi]
             )
-            nc.sync.dma_start(word_rows[:, lo:hi], out_codes[:, lo:hi])
 
         for lo, hi in ((0, P), (P, CHUNK), (CHUNK, HALF)):
             last_look_up(lo, hi)
             round_high(lo, hi, nc.scalar.copy)
-        nc.sync.dma_start(out_rows[:, 3, 0:HALF], high[:, J : J + HALF])
         last_look_up(HALF, HALF + CHUNK)
         round_high(HALF, HALF + CHUNK, nc.scalar.copy)
         last_look_up(HALF + CHUNK, J)
-        round_high(HALF + CHUNK, J - P, nc.scalar.copy)
-        nc.sync.dma_start(out_rows[:, 3, HALF:J], high[:, J + HALF : 2 * J])
-        quantize_out(0, HALF)
-        round_high(J - P, J, nc.vector.tensor_copy)
-        quantize_out(HALF, HALF + CHUNK)
-        quantize_out(HALF + CHUNK, J)
+        nc.sync.dma_start(out_rows[:, 3, :], high[:, J : 2 * J])
+        quantize_out(0, CHUNK)
+        round_high(HALF + CHUNK, J, nc.vector.tensor_copy)
+        quantize_out(CHUNK, HALF)
+        nc.sync.dma_start(word_rows[:, 0:HALF], out_codes[:, 0:HALF])
+        quantize_out(HALF, J)
+        nc.sync.dma_start(word_rows[:, HALF:J], out_codes[:, HALF:J])
         for q in QUADRANTS:
             queue = nc.scalar if q < 2 else nc.sync
             queue.dma_start(out_2[0, 4 * q : 4 * q + 4, :].bitcast(I32), out_scales[32 * q : 32 * q + 4, :].bitcast(I32))

@@ -32,10 +32,11 @@ QUADRANTS = (0, 2, 1, 3)
 WORD_BYTES = 4 * R
 GATE_BYTES = 4 * T
 OVERLAP = 4096
-SECOND_AT = 3 * WORD_BYTES // 2
-WU1_AT = SECOND_AT + WORD_BYTES
+WU0_AT = WORD_BYTES
+WU1_AT = WU0_AT + 3 * WORD_BYTES
 LATE_AT = WU1_AT + 4 * P
-GATE0_AT = 5 * WORD_BYTES
+WD_RAW_AT = WU1_AT + 2 * WORD_BYTES
+GATE0_AT = WD_RAW_AT + WORD_BYTES
 GATE1_AT = GATE0_AT + GATE_BYTES
 TABLE_AT = GATE1_AT + GATE_BYTES - OVERLAP
 GATE2_AT = TABLE_AT + GATE_BYTES - OVERLAP
@@ -98,7 +99,7 @@ def tile_list_gmlpt_gelu_gateP_kernel(
             first = ROWS_AT + 8 * q
             nc.sync.dma_start(planes[32 * q : 32 * q + 4, :, :].bitcast(I32), staged[first : first + 8, :].bitcast(I32))
 
-        unread = psum.tile([P, R], F32, name="unread", tag="y", bufs=3)
+        unread = psum.tile([P, R], F32, name="unread", tag="y", bufs=2)
         for repeat in range(2):
             nc.tensor.matmul_mx(
                 out=unread[:],
@@ -111,9 +112,11 @@ def tile_list_gmlpt_gelu_gateP_kernel(
             )
 
         wg1_raw = load_words("wg1_raw", wg_words[1], 0)
-        wu0_raw = load_words("wu0_raw", wu_words[0], WORD_BYTES)
+        wu0_wide = shared.tile([P, 3 * R], I32, name="wu0_wide", offset=WU0_AT, align_bytes=64)
+        wu0_raw = wu0_wide[:, 0:R]
+        nc.sync.dma_start(wu0_raw, wu_words[0].rearrange("p r i -> p (r i)").bitcast(I32))
         wu1_raw = load_words("wu1_raw", wu_words[1], WU1_AT)
-        wd_raw = shared.tile([P, N // 2], I32, name="wd_raw", offset=4 * WORD_BYTES, align_bytes=64)
+        wd_raw = shared.tile([P, N // 2], I32, name="wd_raw", offset=WD_RAW_AT, align_bytes=64)
         nc.sync.dma_start(wd_raw[:], wd_words[0].bitcast(I32))
 
         def gather_pairs(pairs, start, count):
@@ -189,7 +192,7 @@ def tile_list_gmlpt_gelu_gateP_kernel(
                 )
 
         def new_bank(w):
-            return psum.tile([P, 4, P], F32, name="sum%d" % w, bufs=2 + w)
+            return psum.tile([P, 4, P], F32, name="sum%d" % w, bufs=3)
 
         def in_pairs(bank):
             return bank[:].rearrange("p t (o i) -> p o t i", i=2)
@@ -225,7 +228,7 @@ def tile_list_gmlpt_gelu_gateP_kernel(
 
         def y_sums(c, slices):
             codes, scales = quantized[c]
-            y = psum.tile([P, 2, CHUNK], F32, name="y", bufs=3)
+            y = psum.tile([P, 2, CHUNK], F32, name="y", bufs=2)
             for i, t in enumerate(slices):
                 nc.tensor.matmul_mx(
                     out=y[:, i, :],
@@ -245,7 +248,7 @@ def tile_list_gmlpt_gelu_gateP_kernel(
                 y_of[t, c] = y_rows[:, i * CHUNK : (i + 1) * CHUNK]
 
         y_of = {}
-        work = held.tile([P, 17 * P], F32, name="work", align_bytes=64)
+        work = held.tile([P, 20 * P], F32, name="work", align_bytes=64)
 
         def cells(first, count):
             return work[:, first * P : (first + count) * P]
@@ -274,12 +277,13 @@ def tile_list_gmlpt_gelu_gateP_kernel(
         def round_low(c):
             nc.scalar.copy(by_pair[:, chunk(c), 0:2], low[:].rearrange("p (t j) -> p j t", t=2)[:, chunk(c), :])
 
-        first = shared.tile([P, 2 * CHUNK], F32, name="first", offset=WORD_BYTES // 2, align_bytes=64)
-        second = shared.tile([P, 2 * CHUNK], F32, name="second", offset=SECOND_AT, align_bytes=64)
-        activated = [first[:], second[:]]
-        activated.extend((own("activated2", 2), cells(6, 4), own("activated4", 2), own("activated5", 2)))
-        activated.extend((span(low, 2, 2), span(low, 6, 2)))
-        h_chunks = [own("h0", 2), cells(0, 4), cells(4, 4), cells(10, 4)]
+        early = [
+            shared.tile([P, 2 * CHUNK], F32, name="early%d" % jt, offset=WU0_AT + jt * WORD_BYTES, align_bytes=64)
+            for jt in range(3)
+        ]
+        activated = [tile[:] for tile in early]
+        activated.extend((own("activated3", 2), cells(2, 4), cells(6, 4), own("activated6", 2), span(low, 6, 2)))
+        h_chunks = [own("h0", 2), own("h1", 2), cells(0, 4), cells(8, 4)]
         h_chunks = [h.bitcast(BF16) for h in h_chunks]
 
         def h_of(jt):
@@ -304,50 +308,52 @@ def tile_list_gmlpt_gelu_gateP_kernel(
         out_rows = out_0.rearrange("(p t) j -> p t j", t=4)
         word_rows = out_1[0].rearrange("p j i -> p (j i)").bitcast(I32)
 
-        banks = [new_bank(0) for jt in range(2)]
-        passes(banks[0], 0, 0, 0)
-        passes(banks[1], 0, 1, 0)
-        passes(banks[0], 0, 0, 1)
-        gelu(banks[0], activated[0])
-        up(0)
-        wd = shared.tile([P, 4, 2 * P], U8, name="wd", offset=WORD_BYTES // 2, align_bytes=64)
+        banks = [new_bank(0) for jt in range(3)]
+        for jt in range(3):
+            passes(banks[jt], 0, jt, 0)
+        for jt in range(2):
+            passes(banks[jt], 0, jt, 1)
+            gelu(banks[jt], activated[jt])
+        first_up = new_bank(1)
+        passes(first_up, 1, 0, 0)
+        passes(banks[2], 0, 2, 1)
+        gelu(banks[2], activated[2])
+        passes(first_up, 1, 0, 1)
+        h_product(first_up, activated[0], h_of(0))
+        wd = shared.tile([P, 4, 2 * P], U8, name="wd", offset=WU0_AT, align_bytes=64)
         nc.scalar.copy(wd[:].bitcast(U16), wd_raw[:].bitcast(U16).rearrange("p (m t) -> p t m", t=4))
-        passes(banks[1], 0, 1, 1)
-        gelu(banks[1], activated[1])
         up(1)
         quantize_h(0, h_chunks[0])
-        tile_sums(2)
+        up(2)
+        gate_sum(3, activated[3])
         y0 = y_sums(0, (0, 1))
-        nc.scalar.copy(cells(3, 14).rearrange("p (i x) -> p i x", i=2)[:, :, 0:CHUNK], y0[:])
-        y_of[0, 0], y_of[1, 0] = cells(3, 2), cells(10, 2)
+        nc.scalar.copy(cells(0, 20).rearrange("p (i x) -> p i x", i=2)[:, :, 0:CHUNK], y0[:])
+        y_of[0, 0], y_of[1, 0] = cells(0, 2), cells(10, 2)
+        up(3)
         second_stage(0, (2, 3), own("y_high0", 2))
+        quantize_h(1, h_chunks[1])
+        look_up(0, 0)
         ahead3 = own("ahead3", 1)
         gather_ahead(3, ahead3)
-        look_up(0, 0)
-        ahead2 = own("ahead2", 1)
-        gather_ahead(2, ahead2)
-        tile_sums(3)
         tile_sums(4)
-        quantize_h(1, h_chunks[1])
-        second_stage(1, (1, 0), cells(12, 4))
+        second_stage(1, (1, 0), span(low, 2, 2))
+        look_up(0, 1)
+        tile_sums(5)
         cross = own("cross", 3)
         second_stage(1, (3, 2), span(cross, 0, 2))
-        tile_sums(5)
-        look_up(0, 1)
+        tile_sums(6)
+        gate_sum(7, activated[7])
         quantize_h(2, h_chunks[2])
-        gate_sum(6, activated[6])
         look_up(1, 0)
         look_up(1, 1)
+        second_stage(2, (0, 1), own("y_low2", 2))
+        second_stage(2, (2, 3), own("y_high2", 2))
+        up(7)
+        look_up(0, 2)
         round_low(0)
         round_low(1)
-        up(6)
-        y2 = low_late(2, own("y_one2", 1))
-        second_stage(2, (2, 3), own("y_high2", 2))
-        tile_sums(7)
-        nc.vector.tensor_tensor(product(0, 2), y2[:, 0, :], ahead2, MULT)
         quantize_h(3, h_chunks[3])
         look_up(1, 2)
-        round_low(2)
         look_up(2, 0)
         y3 = low_late(3, y_of[2, 0])
         look_up(2, 1)
@@ -355,6 +361,7 @@ def tile_list_gmlpt_gelu_gateP_kernel(
         nc.vector.tensor_tensor(product(0, 3), y3[:, 0, :], ahead3, MULT)
         nc.sync.dma_start(out_rows[:, 0, :], low[:, 0:J])
         look_up(1, 3)
+        round_low(2)
         round_low(3)
         nc.sync.dma_start(out_rows[:, 1, :], low[:, J : 2 * J])
         for c in range(2, CHUNKS):

@@ -26,7 +26,6 @@ WG_AT = J
 WU_AT = WG_AT + R
 WD_AT = WU_AT + R
 PLANES = WD_AT + N // 2
-ROWS_AT = 96
 QUADRANTS = (0, 2, 1, 3)
 
 WORD_BYTES = 4 * R
@@ -62,16 +61,25 @@ def tile_list_gmlpt_gelu_gateP_kernel(
         def chunk(c):
             return slice(c * CHUNK, (c + 1) * CHUNK)
 
-        rows = slice(ROWS_AT, P)
+        def load_words(raw, source):
+            nc.sync.dma_start(raw, source.rearrange("p r i -> p (r i)").bitcast(I32))
+
+        wd_raw = held.tile([P, N // 2], I32, name="wd_raw", align_bytes=64)
+        nc.scalar.dma_start(wd_raw[:], wd_words[0].bitcast(I32))
+        wg0_raw = held.tile([P, R], I32, name="wg0_raw", align_bytes=64)
+        load_words(wg0_raw[:], wg_words[0])
+
+        rows = slice(0, P, 4)
         table_scales = held.tile([P, T], U8, name="table_scales", align_bytes=64)
-        nc.sync.dma_start(table_scales[rows, :].bitcast(I32), tab_scales.rearrange("a b t -> b a t").bitcast(I32))
         wg_rows = held.tile([P, R], U8, name="wg_rows", align_bytes=64)
         staged = held.tile([P, PLANES], U8, name="staged", align_bytes=64)
-        nc.scalar.dma_start(wg_rows[rows, :].bitcast(I32), wg_scales.rearrange("a b r -> b a r").bitcast(I32))
+        nc.gpsimd.memset(table_scales[:, 0 : T // 2].bitcast(I32), 0)
+        nc.vector.memset(wg_rows[:].bitcast(I32), 0)
+        nc.vector.memset(table_scales[:, T // 2 : T].bitcast(I32), 0)
         nc.scalar.dma_start(staged[rows, WU_AT:WD_AT].bitcast(I32), wu_scales.rearrange("a b r -> b a r").bitcast(I32))
-        nc.sync.dma_start(staged[rows, WD_AT:PLANES].bitcast(I32), wd_scales[0].rearrange("b (h n) -> (b h) n", h=2).bitcast(I32))
-        nc.vector.memset(wg_rows[0:ROWS_AT, :].bitcast(I32), 0)
-        nc.vector.memset(table_scales[0:ROWS_AT, :].bitcast(I32), 0)
+        nc.scalar.dma_start(staged[rows, WD_AT:PLANES].bitcast(I32), wd_scales[0].rearrange("b (h n) -> (b h) n", h=2).bitcast(I32))
+        nc.sync.dma_start(table_scales[rows, :].bitcast(I32), tab_scales.rearrange("a b t -> b a t").bitcast(I32))
+        nc.scalar.dma_start(wg_rows[rows, :].bitcast(I32), wg_scales.rearrange("a b r -> b a r").bitcast(I32))
         zero = held.tile([P, 2], F32, name="zero")
         nc.gpsimd.memset(zero[:, 0:1], 0.0)
         nc.scalar.activation(zero[:, 1:2], zero[:, 0:1], GELU)
@@ -81,12 +89,10 @@ def tile_list_gmlpt_gelu_gateP_kernel(
         table = shared.tile([P, T], I32, name="table", offset=TABLE_AT, align_bytes=64)
         nc.sync.dma_start(table[:], tab_words[0].rearrange("p t b -> p (t b)").bitcast(I32))
 
-        def load_words(name, source, at):
-            raw = shared.tile([P, R], I32, name=name, offset=at, align_bytes=64)
-            nc.sync.dma_start(raw[:], source.rearrange("p r i -> p (r i)").bitcast(I32))
-            return raw
-
-        wg0_raw = load_words("wg0_raw", wg_words[0], PAIRS_AT + WORD_BYTES)
+        wg1_raw = held.tile([P, R], I32, name="wg1_raw", align_bytes=64)
+        load_words(wg1_raw[:], wg_words[1])
+        wd = held.tile([P, 4, 2 * P], U8, name="wd", align_bytes=64)
+        nc.scalar.copy(wd[:].bitcast(U16), wd_raw[:].bitcast(U16).rearrange("p (m t) -> p t m", t=4))
 
         nc.vector.tensor_copy(
             staged[:, WG_AT:WU_AT].rearrange("p (t m) -> p t m", t=4),
@@ -96,28 +102,25 @@ def tile_list_gmlpt_gelu_gateP_kernel(
         nc.vector.tensor_copy(picked_rows[:, 0:J], table_scales[:].indirect(offsets[:]))
         nc.vector.tensor_copy(staged[:, 0:J].bitcast(I32), picked_rows[:, 0:J].bitcast(I32))
         for q in QUADRANTS:
-            first = ROWS_AT + 8 * q
-            nc.sync.dma_start(planes[32 * q : 32 * q + 4, :, :].bitcast(I32), staged[first : first + 8, :].bitcast(I32))
+            nc.sync.dma_start(planes[32 * q : 32 * q + 4, :, :].bitcast(I32), staged[32 * q : 32 * q + 32 : 4, :].bitcast(I32))
 
         unread = psum.tile([P, R], F32, name="unread", tag="y", bufs=2)
         for repeat in range(2):
             nc.tensor.matmul_mx(
                 out=unread[:],
-                lhsT=wg0_raw[:, 0 : P // 2].bitcast(FP4X4),
+                lhsT=wg1_raw[:, 0 : P // 2].bitcast(FP4X4),
                 lhsT_scale=staged[:, 0:P],
-                rhs=wg0_raw[:].bitcast(FP8X4),
+                rhs=wg1_raw[:].bitcast(FP8X4),
                 rhs_scale=staged[:, 0:R],
                 start=True,
                 stop=True,
             )
 
-        wg1_raw = load_words("wg1_raw", wg_words[1], 0)
         wu0_wide = shared.tile([P, 3 * R], I32, name="wu0_wide", offset=WU0_AT, align_bytes=64)
         wu0_raw = wu0_wide[:, 0:R]
         nc.sync.dma_start(wu0_raw, wu_words[0].rearrange("p r i -> p (r i)").bitcast(I32))
-        wu1_raw = load_words("wu1_raw", wu_words[1], WU1_AT)
-        wd_raw = shared.tile([P, N // 2], I32, name="wd_raw", offset=WD_RAW_AT, align_bytes=64)
-        nc.sync.dma_start(wd_raw[:], wd_words[0].bitcast(I32))
+        wu1_raw = shared.tile([P, R], I32, name="wu1_raw", offset=WU1_AT, align_bytes=64)
+        load_words(wu1_raw[:], wu_words[1])
 
         def gather_pairs(pairs, start, count):
             nc.vector.tensor_copy(pairs[:], table[:].bitcast(U32).indirect(entries(start, count)))
@@ -308,23 +311,15 @@ def tile_list_gmlpt_gelu_gateP_kernel(
         out_rows = out_0.rearrange("(p t) j -> p t j", t=4)
         word_rows = out_1[0].rearrange("p j i -> p (j i)").bitcast(I32)
 
-        banks = [new_bank(0) for jt in range(3)]
-        for jt in range(3):
-            passes(banks[jt], 0, jt, 0)
+        banks = [new_bank(0) for jt in range(2)]
         for jt in range(2):
-            passes(banks[jt], 0, jt, 1)
+            for a in range(PASSES):
+                passes(banks[jt], 0, jt, a)
             gelu(banks[jt], activated[jt])
-        first_up = new_bank(1)
-        passes(first_up, 1, 0, 0)
-        passes(banks[2], 0, 2, 1)
-        gelu(banks[2], activated[2])
-        passes(first_up, 1, 0, 1)
-        h_product(first_up, activated[0], h_of(0))
-        wd = shared.tile([P, 4, 2 * P], U8, name="wd", offset=WU0_AT, align_bytes=64)
-        nc.scalar.copy(wd[:].bitcast(U16), wd_raw[:].bitcast(U16).rearrange("p (m t) -> p t m", t=4))
+        up(0)
         up(1)
         quantize_h(0, h_chunks[0])
-        up(2)
+        tile_sums(2)
         gate_sum(3, activated[3])
         y0 = y_sums(0, (0, 1))
         nc.scalar.copy(cells(0, 20).rearrange("p (i x) -> p i x", i=2)[:, :, 0:CHUNK], y0[:])

@@ -31,11 +31,8 @@ QUADRANTS = (0, 2, 1, 3)
 WORD_BYTES = 4 * R
 GATE_BYTES = 4 * T
 OVERLAP = 4096
-WU0_AT = WORD_BYTES
-WU1_AT = WU0_AT + 3 * WORD_BYTES
-LATE_AT = WU1_AT + 4 * P
-WD_RAW_AT = WU1_AT + 2 * WORD_BYTES
-GATE0_AT = WD_RAW_AT + WORD_BYTES
+LATE_AT = 3 * WORD_BYTES
+GATE0_AT = 5 * WORD_BYTES
 GATE1_AT = GATE0_AT + GATE_BYTES
 TABLE_AT = GATE1_AT + GATE_BYTES - OVERLAP
 GATE2_AT = TABLE_AT + GATE_BYTES - OVERLAP
@@ -116,11 +113,10 @@ def tile_list_gmlpt_gelu_gateP_kernel(
                 stop=True,
             )
 
-        wu0_wide = shared.tile([P, 3 * R], I32, name="wu0_wide", offset=WU0_AT, align_bytes=64)
-        wu0_raw = wu0_wide[:, 0:R]
-        nc.sync.dma_start(wu0_raw, wu_words[0].rearrange("p r i -> p (r i)").bitcast(I32))
-        wu1_raw = shared.tile([P, R], I32, name="wu1_raw", offset=WU1_AT, align_bytes=64)
-        load_words(wu1_raw[:], wu_words[1])
+        wu_raw = shared.tile([P, 4 * R + P], I32, name="wu_raw", offset=0, align_bytes=64)
+        nc.sync.dma_start(
+            wu_raw[:, 0 : PASSES * R].rearrange("p (a r) -> p a r", a=PASSES), wu_words.rearrange("a p r i -> p a (r i)").bitcast(I32)
+        )
 
         def gather_pairs(pairs, start, count):
             nc.vector.tensor_copy(pairs[:], table[:].bitcast(U32).indirect(entries(start, count)))
@@ -152,16 +148,16 @@ def tile_list_gmlpt_gelu_gateP_kernel(
         late_pairs = shared.tile([P, HALF], U32, name="late_pairs", offset=PAIRS_AT, align_bytes=64)
         gather_pairs(late_pairs, HALF, HALF)
         wg1 = deal("wg1", wg1_raw, nc.scalar.copy)
-        wu0 = deal("wu0", wu0_raw, nc.scalar.copy)
         wu_scale = held.tile([P, PASSES, R], U8, name="wu_scale", align_bytes=64)
         nc.vector.tensor_copy(
             wu_scale[:].rearrange("p a (t m) -> p a t m", t=4),
             planes[:, :, WU_AT:WD_AT].rearrange("p a (m t) -> p a t m", t=4),
         )
-        wu1 = deal("wu1", wu1_raw, nc.vector.tensor_copy)
+        wu0 = deal("wu0", wu_raw[:, 0:R], nc.vector.tensor_copy)
+        wu1 = deal("wu1", wu_raw[:, R : 2 * R], nc.scalar.copy)
         late_words = shared.tile([P, PASSES, 2 * HALF], U8, name="late_words", offset=LATE_AT, align_bytes=64)
         part(late_words, late_pairs)
-        wd_scale = shared.tile([P, 4, P], U8, name="wd_scale", offset=WU1_AT, align_bytes=64)
+        wd_scale = shared.tile([P, 4, P], U8, name="wd_scale", offset=LATE_AT + WORD_BYTES, align_bytes=64)
         nc.vector.tensor_copy(
             wd_scale[:].rearrange("p t (h m) -> p t h m", h=2),
             planes[:, :, WD_AT:PLANES].rearrange("p h (m t) -> p t h m", t=4),
@@ -281,7 +277,7 @@ def tile_list_gmlpt_gelu_gateP_kernel(
             nc.scalar.copy(by_pair[:, chunk(c), 0:2], low[:].rearrange("p (t j) -> p j t", t=2)[:, chunk(c), :])
 
         early = [
-            shared.tile([P, 2 * CHUNK], F32, name="early%d" % jt, offset=WU0_AT + jt * WORD_BYTES, align_bytes=64)
+            shared.tile([P, 2 * CHUNK], F32, name="early%d" % jt, offset=jt * WORD_BYTES, align_bytes=64)
             for jt in range(3)
         ]
         activated = [tile[:] for tile in early]

from contextlib import ExitStack

import concourse.mybir as mybir

K, R, N, T, J = 1024, 512, 512, 4096, 1024
FLOPS = 2 * J * (2 * K * R + R * N)

F32 = mybir.dt.float32
BF16 = mybir.dt.bfloat16
I32 = mybir.dt.int32
U32 = mybir.dt.uint32
U16 = mybir.dt.uint16
U8 = mybir.dt.uint8
FP8X4 = mybir.dt.float8_e4m3fn_x4
FP4X4 = mybir.dt.float4_e2m1fn_x4
MULT = mybir.AluOpType.mult
GELU = mybir.ActivationFunctionType.Gelu_apprx_tanh

P = 128
PASSES = K // 512
HALF = J // 2
CHUNK = 256
CHUNKS = J // CHUNK

WG_AT = J
WU_AT = WG_AT + R
WD_AT = WU_AT + R
PLANES = WD_AT + N // 2
QUADRANTS = (0, 2, 1, 3)

WORD_BYTES = 4 * R
GATE_BYTES = 4 * T
OVERLAP = 4096
LATE_AT = 3 * WORD_BYTES
GATE0_AT = 5 * WORD_BYTES
GATE1_AT = GATE0_AT + GATE_BYTES
TABLE_AT = GATE1_AT + GATE_BYTES - OVERLAP
GATE2_AT = TABLE_AT + GATE_BYTES - OVERLAP
GATE3_AT = GATE2_AT + GATE_BYTES
PAIRS_AT = GATE3_AT + GATE_BYTES - WORD_BYTES


def tile_list_gmlpt_gelu_gateP_kernel(
    tc, tab_words, tab_scales, wg_words, wg_scales, wu_words, wu_scales, wd_words, wd_scales, gT, offs, out_0, out_1, out_2
):
    nc = tc.nc
    with ExitStack() as ctx:
        held = ctx.enter_context(tc.tile_pool(name="held", bufs=1))
        shared = ctx.enter_context(tc.tile_pool(name="shared", bufs=1))
        psum = ctx.enter_context(tc.psum_pool(name="psum", bufs=1))

        offsets = held.tile([P, J // 16], U16, name="offsets")
        nc.sync.dma_start(offsets[:], offs)

        def entries(start, count):
            return offsets[:, start // 16 : (start + count) // 16]

        def chunk(c):
            return slice(c * CHUNK, (c + 1) * CHUNK)

        def load_words(raw, source):
            nc.sync.dma_start(raw, source.rearrange("p r i -> p (r i)").bitcast(I32))

        wd_raw = held.tile([P, N // 2], I32, name="wd_raw", align_bytes=64)
        nc.scalar.dma_start(wd_raw[:], wd_words[0].bitcast(I32))
        wg0_raw = held.tile([P, R], I32, name="wg0_raw", align_bytes=64)
        load_words(wg0_raw[:], wg_words[0])

        rows = slice(0, P, 4)
        table_scales = held.tile([P, T], U8, name="table_scales", align_bytes=64)
        wg_rows = held.tile([P, R], U8, name="wg_rows", align_bytes=64)
        staged = held.tile([P, PLANES], U8, name="staged", align_bytes=64)
        nc.gpsimd.memset(table_scales[:, 0 : T // 2].bitcast(I32), 0)
        nc.vector.memset(wg_rows[:].bitcast(I32), 0)
        nc.vector.memset(table_scales[:, T // 2 : T].bitcast(I32), 0)
        nc.scalar.dma_start(staged[rows, WU_AT:WD_AT].bitcast(I32), wu_scales.rearrange("a b r -> b a r").bitcast(I32))
        nc.scalar.dma_start(staged[rows, WD_AT:PLANES].bitcast(I32), wd_scales[0].rearrange("b (h n) -> (b h) n", h=2).bitcast(I32))
        nc.sync.dma_start(table_scales[rows, :].bitcast(I32), tab_scales.rearrange("a b t -> b a t").bitcast(I32))
        nc.scalar.dma_start(wg_rows[rows, :].bitcast(I32), wg_scales.rearrange("a b r -> b a r").bitcast(I32))
        zero = held.tile([P, 2], F32, name="zero")
        nc.gpsimd.memset(zero[:, 0:1], 0.0)
        nc.scalar.activation(zero[:, 1:2], zero[:, 0:1], GELU)
        planes = held.tile([P, PASSES, PLANES], U8, name="planes", align_bytes=64)
        nc.vector.memset(planes[:].bitcast(I32), 0)

        table = shared.tile([P, T], I32, name="table", offset=TABLE_AT, align_bytes=64)
        nc.sync.dma_start(table[:], tab_words[0].rearrange("p t b -> p (t b)").bitcast(I32))

        wg1_raw = held.tile([P, R], I32, name="wg1_raw", align_bytes=64)
        load_words(wg1_raw[:], wg_words[1])
        wd = held.tile([P, 4, 2 * P], U8, name="wd", align_bytes=64)
        nc.scalar.copy(wd[:].bitcast(U16), wd_raw[:].bitcast(U16).rearrange("p (m t) -> p t m", t=4))

        nc.vector.tensor_copy(
            staged[:, WG_AT:WU_AT].rearrange("p (t m) -> p t m", t=4),
            wg_rows[:].rearrange("p (m t) -> p t m", t=4),
        )
        picked_rows = shared.tile([P, GATE0_AT + 64], U8, name="picked_rows", offset=0, align_bytes=64)
        nc.vector.tensor_copy(picked_rows[:, 0:J], table_scales[:].indirect(offsets[:]))
        nc.vector.tensor_copy(staged[:, 0:J].bitcast(I32), picked_rows[:, 0:J].bitcast(I32))
        for q in QUADRANTS:
            nc.sync.dma_start(planes[32 * q : 32 * q + 4, :, :].bitcast(I32), staged[32 * q : 32 * q + 32 : 4, :].bitcast(I32))

        unread = psum.tile([P, R], F32, name="unread", tag="y", bufs=2)
        for repeat in range(2):
            nc.tensor.matmul_mx(
                out=unread[:],
                lhsT=wg1_raw[:, 0 : P // 2].bitcast(FP4X4),
                lhsT_scale=staged[:, 0:P],
                rhs=wg1_raw[:].bitcast(FP8X4),
                rhs_scale=staged[:, 0:R],
                start=True,
                stop=True,
            )

        wu_raw = shared.tile([P, 4 * R + P], I32, name="wu_raw", offset=0, align_bytes=64)
        nc.sync.dma_start(
            wu_raw[:, 0 : PASSES * R].rearrange("p (a r) -> p a r", a=PASSES), wu_words.rearrange("a p r i -> p a (r i)").bitcast(I32)
        )

        def gather_pairs(pairs, start, count):
            nc.vector.tensor_copy(pairs[:], table[:].bitcast(U32).indirect(entries(start, count)))

        def part(words, pairs):
            nc.vector.tensor_copy(
                words[:].bitcast(U16).rearrange("p a (o i) -> p o a i", i=8),
                pairs[:].bitcast(U16).rearrange("p (o i a) -> p o a i", a=PASSES, i=8),
            )

        def deal(name, raw, copy):
            dealt = held.tile([P, R], U32, name=name, align_bytes=64)
            copy(
                dealt[:].rearrange("p (t m) -> p m t", t=4),
                raw[:, :].bitcast(U32).rearrange("p (m t) -> p m t", t=4),
            )
            return dealt

        pairs = [
            shared.tile([P, CHUNK], U32, name="pairs0", offset=PAIRS_AT, align_bytes=64),
            held.tile([P, CHUNK], U32, name="pairs1", align_bytes=64),
        ]
        words = [held.tile([P, PASSES, 2 * CHUNK], U8, name="words%d" % c, align_bytes=64) for c in range(2)]
        gather_pairs(pairs[0], 0, CHUNK)
        gather_pairs(pairs[1], CHUNK, CHUNK)
        part(words[0], pairs[0])
        wg0 = deal("wg0", wg0_raw, nc.scalar.copy)
        part(words[1], pairs[1])
        late_pairs = shared.tile([P, HALF], U32, name="late_pairs", offset=PAIRS_AT, align_bytes=64)
        gather_pairs(late_pairs, HALF, HALF)
        wg1 = deal("wg1", wg1_raw, nc.scalar.copy)
        wu_scale = held.tile([P, PASSES, R], U8, name="wu_scale", align_bytes=64)
        nc.vector.tensor_copy(
            wu_scale[:].rearrange("p a (t m) -> p a t m", t=4),
            planes[:, :, WU_AT:WD_AT].rearrange("p a (m t) -> p a t m", t=4),
        )
        wu0 = deal("wu0", wu_raw[:, 0:R], nc.vector.tensor_copy)
        wu1 = deal("wu1", wu_raw[:, R : 2 * R], nc.scalar.copy)
        late_words = shared.tile([P, PASSES, 2 * HALF], U8, name="late_words", offset=LATE_AT, align_bytes=64)
        part(late_words, late_pairs)
        wd_scale = shared.tile([P, 4, P], U8, name="wd_scale", offset=LATE_AT + WORD_BYTES, align_bytes=64)
        nc.vector.tensor_copy(
            wd_scale[:].rearrange("p t (h m) -> p t h m", h=2),
            planes[:, :, WD_AT:PLANES].rearrange("p h (m t) -> p t h m", t=4),
        )
        weight_scales = (planes[:, :, WG_AT:WU_AT], wu_scale[:])
        weights = ((wg0, wg1), (wu0, wu1))

        gate_rows = gT.rearrange("(p t) c -> t p c", t=4)
        gates = [
            shared.tile([P, T], F32, name="gate%d" % t, offset=at, align_bytes=64)
            for t, at in enumerate((GATE0_AT, GATE1_AT, GATE2_AT, GATE3_AT))
        ]
        for t in range(4):
            nc.sync.dma_start(gates[t][:], gate_rows[t])

        def picked(jt, a):
            if jt < 4:
                return words[jt // 2][:, a, 2 * P * (jt % 2) : 2 * P * (jt % 2 + 1)]
            return late_words[:, a, 2 * P * (jt - 4) : 2 * P * (jt - 3)]

        def passes(bank, w, jt, a):
            for t in range(4):
                nc.tensor.matmul_mx(
                    out=bank[:, t, :],
                    lhsT=weights[w][a][:, t * P : (t + 1) * P].bitcast(FP8X4),
                    lhsT_scale=weight_scales[w][:, a, t * P : (t + 1) * P],
                    rhs=picked(jt, a).bitcast(FP4X4),
                    rhs_scale=planes[:, a, jt * P : (jt + 1) * P],
                    start=(a == 0 and t == 0),
                    stop=(a == PASSES - 1 and t == 3),
                )

        def new_bank(w):
            return psum.tile([P, 4, P], F32, name="sum%d" % w, bufs=3)

        def in_pairs(bank):
            return bank[:].rearrange("p t (o i) -> p o t i", i=2)

        def as_read(flat):
            return flat.rearrange("p (o t i) -> p o t i", t=4, i=2)

        def gelu(bank, activated):
            nc.scalar.activation(as_read(activated), in_pairs(bank), GELU)

        def gate_sum(jt, activated):
            bank = new_bank(0)
            for a in range(PASSES):
                passes(bank, 0, jt, a)
            gelu(bank, activated)

        def up_sum(jt):
            bank = new_bank(1)
            for a in range(PASSES):
                passes(bank, 1, jt, a)
            return bank

        def h_product(bank, activated, h):
            nc.vector.tensor_tensor(h.rearrange("p (o i t) -> p o t i", t=4, i=2), in_pairs(bank), as_read(activated), MULT)

        quantized = []

        def quantize_h(c, h):
            codes = held.tile([P, CHUNK], U32, name="h_codes%d" % c, align_bytes=64)
            scales = held.tile([P, CHUNK], U8, name="h_scales%d" % c, align_bytes=64)
            nc.vector.quantize_mx(out=codes[:].bitcast(FP8X4), scales=scales[:], in_=h)
            quantized.append((codes, scales))

        def y_sums(c, slices):
            codes, scales = quantized[c]
            y = psum.tile([P, 2, CHUNK], F32, name="y", bufs=2)
            for i, t in enumerate(slices):
                nc.tensor.matmul_mx(
                    out=y[:, i, :],
                    lhsT=wd[:, t, :].bitcast(FP4X4),
                    lhsT_scale=wd_scale[:, t, :],
                    rhs=codes[:].bitcast(FP8X4),
                    rhs_scale=scales[:],
                    start=True,
                    stop=True,
                )
            return y

        def second_stage(c, slices, y_rows):
            y = y_sums(c, slices)
            nc.scalar.copy(y_rows, y[:].rearrange("p i j -> p (i j)"))
            for i, t in enumerate(slices):
                y_of[t, c] = y_rows[:, i * CHUNK : (i + 1) * CHUNK]

        y_of = {}
        work = held.tile([P, 20 * P], F32, name="work", align_bytes=64)

        def cells(first, count):
            return work[:, first * P : (first + count) * P]

        low = held.tile([P, 2 * J], F32, name="low", align_bytes=64)
        high = held.tile([P, 2 * J], F32, name="high", align_bytes=64)

        def span(tile, first, count):
            return tile[:, first * CHUNK : (first + count) * CHUNK]

        def product(t, c):
            if t < 2:
                return span(low, 4 * t + c, 1)
            return span(high, 4 * (t - 2) + c, 1)

        def look_up(t, c):
            nc.vector.tensor_tensor(product(t, c), gates[t][:].indirect(entries(c * CHUNK, CHUNK)), y_of[t, c], MULT)

        def own(name, count):
            tile = held.tile([P, count * CHUNK], F32, name=name, align_bytes=64)
            return tile[:]

        rounded = held.tile([P, 4 * J], BF16, name="rounded", align_bytes=64)
        by_pair = rounded[:].rearrange("p (j t) -> p j t", t=4)

        def round_low(c):
            nc.scalar.copy(by_pair[:, chunk(c), 0:2], low[:].rearrange("p (t j) -> p j t", t=2)[:, chunk(c), :])

        early = [
            shared.tile([P, 2 * CHUNK], F32, name="early%d" % jt, offset=jt * WORD_BYTES, align_bytes=64)
            for jt in range(3)
        ]
        activated = [tile[:] for tile in early]
        activated.extend((own("activated3", 2), cells(2, 4), cells(6, 4), own("activated6", 2), span(low, 6, 2)))
        h_chunks = [own("h0", 2), own("h1", 2), cells(0, 4), cells(8, 4)]
        h_chunks = [h.bitcast(BF16) for h in h_chunks]

        def h_of(jt):
            return h_chunks[jt // 2][:, (jt % 2) * 4 * P : (jt % 2 + 1) * 4 * P]

        def up(jt):
            h_product(up_sum(jt), activated[jt], h_of(jt))

        def tile_sums(jt):
            gate_sum(jt, activated[jt])
            up(jt)

        def gather_ahead(c, target):
            nc.vector.tensor_copy(target, gates[0][:].indirect(entries(c * CHUNK, CHUNK)))

        def low_late(c, y_row):
            y = y_sums(c, (0, 1))
            nc.scalar.copy(y_row, y[:, 1, :])
            y_of[1, c] = y_row
            return y

        out_rows = out_0.rearrange("(p t) j -> p t j", t=4)
        word_rows = out_1[0].rearrange("p j i -> p (j i)").bitcast(I32)

        banks = [new_bank(0) for jt in range(2)]
        for jt in range(2):
            for a in range(PASSES):
                passes(banks[jt], 0, jt, a)
            gelu(banks[jt], activated[jt])
        up(0)
        up(1)
        quantize_h(0, h_chunks[0])
        tile_sums(2)
        gate_sum(3, activated[3])
        y0 = y_sums(0, (0, 1))
        nc.scalar.copy(cells(0, 20).rearrange("p (i x) -> p i x", i=2)[:, :, 0:CHUNK], y0[:])
        y_of[0, 0], y_of[1, 0] = cells(0, 2), cells(10, 2)
        up(3)
        second_stage(0, (2, 3), own("y_high0", 2))
        quantize_h(1, h_chunks[1])
        look_up(0, 0)
        ahead3 = own("ahead3", 1)
        gather_ahead(3, ahead3)
        tile_sums(4)
        second_stage(1, (1, 0), span(low, 2, 2))
        look_up(0, 1)
        tile_sums(5)
        cross = own("cross", 3)
        second_stage(1, (3, 2), span(cross, 0, 2))
        tile_sums(6)
        gate_sum(7, activated[7])
        quantize_h(2, h_chunks[2])
        look_up(1, 0)
        look_up(1, 1)
        second_stage(2, (0, 1), own("y_low2", 2))
        second_stage(2, (2, 3), own("y_high2", 2))
        up(7)
        look_up(0, 2)
        round_low(0)
        round_low(1)
        quantize_h(3, h_chunks[3])
        look_up(1, 2)
        look_up(2, 0)
        y3 = low_late(3, y_of[2, 0])
        look_up(2, 1)
        second_stage(3, (2, 3), span(cross, 1, 2))
        nc.vector.tensor_tensor(product(0, 3), y3[:, 0, :], ahead3, MULT)
        nc.sync.dma_start(out_rows[:, 0, :], low[:, 0:J])
        look_up(1, 3)
        round_low(2)
        round_low(3)
        nc.sync.dma_start(out_rows[:, 1, :], low[:, J : 2 * J])
        for c in range(2, CHUNKS):
            look_up(2, c)
        nc.sync.dma_start(out_rows[:, 2, :], high[:, 0:J])

        out_codes = held.tile([P, J], I32, name="out_codes", align_bytes=64)
        out_scales = held.tile([P, J], U8, name="out_scales", align_bytes=64)

        high_by_entry = high[:].rearrange("p (t j) -> p j t", t=2)
        y_three = [y_of[3, c] for c in range(CHUNKS)]

        def last_look_up(lo, hi):
            c, col = divmod(lo, CHUNK)
            nc.vector.tensor_tensor(
                high[:, J + lo : J + hi], gates[3][:].indirect(entries(lo, hi - lo)), y_three[c][:, col : col + hi - lo], MULT
            )

        def round_high(lo, hi, copy):
            copy(by_pair[:, lo:hi, 2:4], high_by_entry[:, lo:hi, :])

        def quantize_out(lo, hi):
            nc.vector.quantize_mx(
                out=out_codes[:, lo:hi].bitcast(FP8X4), scales=out_scales[:, lo:hi], in_=rounded[:, 4 * lo : 4 * hi]
            )

        for lo, hi in ((0, P), (P, CHUNK), (CHUNK, HALF)):
            last_look_up(lo, hi)
            round_high(lo, hi, nc.scalar.copy)
        last_look_up(HALF, HALF + CHUNK)
        round_high(HALF, HALF + CHUNK, nc.scalar.copy)
        last_look_up(HALF + CHUNK, J)
        nc.sync.dma_start(out_rows[:, 3, :], high[:, J : 2 * J])
        quantize_out(0, CHUNK)
        round_high(HALF + CHUNK, J, nc.vector.tensor_copy)
        quantize_out(CHUNK, HALF)
        nc.sync.dma_start(word_rows[:, 0:HALF], out_codes[:, 0:HALF])
        quantize_out(HALF, J)
        nc.sync.dma_start(word_rows[:, HALF:J], out_codes[:, HALF:J])
        for q in QUADRANTS:
            queue = nc.scalar if q < 2 else nc.sync
            queue.dma_start(out_2[0, 4 * q : 4 * q + 4, :].bitcast(I32), out_scales[32 * q : 32 * q + 4, :].bitcast(I32))
